import numpy as np
import ml_dtypes


def mxq(x, axis, fmt="e4m3"):
    dtype, down = {"e4m3": (ml_dtypes.float8_e4m3fn, 7), "e5m2": (ml_dtypes.float8_e5m2, 14)}[fmt]
    v = np.moveaxis(np.asarray(x, np.float32).astype(ml_dtypes.bfloat16).astype(np.float64), axis, -1)
    blocks = v.reshape(v.shape[:-1] + (-1, 32))
    amax = np.abs(blocks).max(-1, keepdims=True)
    byte = np.maximum(np.where(amax > 0, np.frexp(amax)[1] - 1 + 127, 0) - down, 1)
    scale = np.exp2(byte - 127.0)
    codes = (blocks / scale).astype(np.float32).astype(dtype).astype(np.float64)
    return np.moveaxis((codes * scale).reshape(v.shape), -1, axis)


WIDE = False


def mx_kscale(k):
    if not WIDE:
        return np.ones(k)
    levels = np.array([10, -10, 5, -5, 0])
    if k % 512:
        return np.exp2(np.random.permutation(np.resize(levels, k // 32))).repeat(32)
    a = np.empty((k // 512, 16))
    for p in range(k // 512):
        a[p, :8] = np.random.permutation(np.resize(levels, 8))
        for g in range(8):
            far = levels[np.abs(levels - a[p, g]) >= 10]
            a[p, g + 8] = far[np.random.randint(len(far))]
    return np.exp2(a.ravel()).repeat(32)


def f64(x):
    return np.asarray(x).astype(np.float64)


def striped(idx):
    return np.tile(idx.reshape(-1, 16).T, (8, 1)).astype(np.uint16)


def unstriped(offs):
    return offs[:16].T.reshape(-1).astype(np.int64)


E2M1 = np.array([0.0, 0.5, 1.0, 1.5, 2.0, 3.0, 4.0, 6.0, -0.0, -0.5, -1.0, -1.5, -2.0, -3.0, -4.0, -6.0])


def pack_weight(w, fmt):
    k, n = w.shape
    w = f64(np.asarray(w, np.float32).astype(ml_dtypes.bfloat16)).reshape(k // 32, 32, n)
    amax = np.abs(w).max(1)
    if fmt == "e4m3":
        byte = np.frexp(amax)[1] - 1 + 127 - 7
    else:
        mant, ex = np.frexp(amax / 6.0)
        byte = np.where(mant > 0.5, ex, ex - 1) + 127
    byte = np.clip(np.where(amax > 0, byte, 1), 1, 254)
    scaled = (w * np.exp2(127.0 - byte)[:, None, :]).reshape(k, n).astype(np.float32)
    by_word = np.ascontiguousarray(scaled.reshape(k // 512, 128, 4, n).transpose(0, 1, 3, 2))
    if fmt == "e4m3":
        words = by_word.astype(ml_dtypes.float8_e4m3fn).view(np.uint8)
    else:
        c = by_word.astype(ml_dtypes.float4_e2m1fn).view(np.uint8) & 0xF
        words = (c[..., 0::2] | (c[..., 1::2] << 4)).reshape(k // 512, 128, 2 * n)
    return np.ascontiguousarray(words), np.ascontiguousarray(byte.astype(np.uint8).reshape(k // 512, 16, n))


def unpack_weight(words, scales, fmt):
    g, _, n = scales.shape
    words = np.ascontiguousarray(words).reshape(g, 128, n, -1)
    if fmt == "e4m3":
        vals = words.view(ml_dtypes.float8_e4m3fn).astype(np.float64)
    else:
        nib = np.empty((g, 128, n, 4), np.uint8)
        nib[..., 0::2] = words & 0xF
        nib[..., 1::2] = words >> 4
        vals = E2M1[nib]
    vals = vals * np.repeat(np.exp2(scales.astype(np.float64) - 127.0), 8, axis=1)[..., None]
    return vals.transpose(0, 1, 3, 2).reshape(g * 512, n)


def gelu(v):
    return 0.5 * v * (1.0 + np.tanh(np.sqrt(2.0 / np.pi) * (v + 0.044715 * v**3)))


K, H, T, S, T2, P = 1536, 1024, 2048, 512, 1024, 512

def setup_inputs():
    n = np.random.standard_normal
    s = mx_kscale(K)[:, None]
    u = mx_kscale(H)[:, None]
    d = {}
    d["tab_words"], d["tab_scales"] = pack_weight(n((K, T)) * s, "e4m3")
    d["offs"] = striped(np.random.permutation(T)[:S])
    d["offs2"] = striped(np.random.permutation(T2)[:S])
    d["offs3"] = striped(np.random.permutation(T2)[:P])
    d["w1"] = (0.7 * n((K, H)) / s * u.T / K ** 0.5).astype(np.float32)
    d["w4_words"], d["w4_scales"] = pack_weight(2.5 * n((K, H)) / s / K ** 0.5, "e2m1")
    d["site"] = (2.0 * n((H, S)) * u).astype(np.float32)
    d["wgs"] = np.exp(0.3 * n((128, S))).astype(np.float32)
    d["page0"] = (1.2 * n((H, T2)) * u).astype(np.float32)
    d["tvec"] = (n(H) / u[:, 0] ** 2 / H ** 0.5).astype(np.float32)
    d["slot"] = (1.5 * np.exp(0.5 * n(T2))).astype(np.float32)
    return d

def reference(tab_words, tab_scales, offs, offs2, offs3, w1, w4_words, w4_scales, site, wgs, page0, tvec, slot):
    v = unpack_weight(tab_words, tab_scales, "e4m3")[:, unstriped(offs)]
    a = mxq(f64(w1), 0, "e4m3").T @ v
    b = unpack_weight(w4_words, w4_scales, "e2m1").T @ v
    gate = 1.0 / (1.0 + np.exp(-b))
    h = a + f64(site) * gate
    page = f64(page0).copy()
    page[:, unstriped(offs2)] = np.tile(f64(wgs), (H // 128, 1)) * h
    x = np.abs(page[:, unstriped(offs3)]) * f64(tvec)[:, None]
    e = mxq(page, 0, "e4m3").T @ mxq(x, 0, "e4m3")
    return e / (np.abs(e) + f64(slot)[:, None])

@@ -1,0 +1,385 @@
+from contextlib import ExitStack
+
+import concourse.mybir as mybir
+from concourse.masks import make_identity
+
+K, H, T, S, T2, NT = 1536, 1024, 2048, 512, 1024, 512
+FLOPS = 2 * (2 * K * H * S + H * T2 * NT)
+
+F32 = mybir.dt.float32
+BF16 = mybir.dt.bfloat16
+I32 = mybir.dt.int32
+U32 = mybir.dt.uint32
+U16 = mybir.dt.uint16
+U8 = mybir.dt.uint8
+E4M3X4 = mybir.dt.float8_e4m3fn_x4
+E2M1X4 = mybir.dt.float4_e2m1fn_x4
+ACT = mybir.ActivationFunctionType
+ALU = mybir.AluOpType
+
+P = 128
+KP = K // 512
+RP = H // 512
+NS = 4 * RP
+CH = 256
+
+
+def tile_list_triage_template_scores_kernel(
+    tc, tab_words, tab_scales, offs, offs2, offs3, w1, w4_words, w4_scales, site, wgs, page0, tvec, slot, out
+):
+    nc = tc.nc
+    with ExitStack() as ctx:
+        keep = ctx.enter_context(tc.tile_pool(name="keep", bufs=1))
+        big = ctx.enter_context(tc.tile_pool(name="big", bufs=6))
+        ring = ctx.enter_context(tc.tile_pool(name="ring", bufs=2))
+        psum = ctx.enter_context(tc.psum_pool(name="psum", bufs=4))
+
+        def kept(shape, dtype, name):
+            return keep.tile(shape, dtype, name=name, align_bytes=64)
+
+        def big_tile(shape, dtype, name):
+            return big.tile(shape, dtype, name=name, tag="big", align_bytes=64)
+
+        def bank(tag, name):
+            return psum.tile([P, 512], F32, name=name, tag=tag)
+
+        def slice_rows(src, s):
+            b, t = divmod(s, 4)
+            return src.rearrange("(b g t i) m -> b t g i m", b=RP, t=4, i=8)[b, t]
+
+        list1 = keep.tile([P, S // 16], U16, name="list1")
+        list2 = keep.tile([P, S // 16], U16, name="list2")
+        list3 = keep.tile([P, NT // 16], U16, name="list3")
+        tab_sc = kept([P, KP, T], U8, "tab_sc")
+        w4_sc_raw = kept([P, KP, H], U8, "w4_sc_raw")
+        vec_rows = kept([P, 2 * P], F32, "vec_rows")
+        ident = kept([P, P], F32, "ident")
+        wgs_nat = kept([P, S], F32, "wgs_nat")
+        nc.vector.memset(tab_sc[:].rearrange("p a t -> p (a t)").bitcast(I32), 0)
+        nc.vector.memset(w4_sc_raw[:].rearrange("p a t -> p (a t)").bitcast(I32), 0)
+        nc.vector.memset(vec_rows[:], 0.0)
+        make_identity(nc, ident[:])
+
+        tab_w, w1_raw, w4_raw, site_sb, page = {}, {}, {}, {}, {}
+
+        def load_tab(a):
+            tab_w[a] = big_tile([P, T], I32, f"tab_w{a}")
+            nc.sync.dma_start(tab_w[a][:], tab_words[a].rearrange("p t i -> p (t i)").bitcast(I32))
+
+        def load_w1(a, b):
+            w1_raw[a, b] = big_tile([P, 4, 512], F32, f"w1_raw{a}{b}")
+            src = w1[512 * a : 512 * (a + 1), 512 * b : 512 * (b + 1)]
+            nc.sync.dma_start(w1_raw[a, b][:], src.rearrange("(p j) c -> p j c", j=4))
+
+        def load_w4(b):
+            w4_raw[b] = kept([P, KP, 256], I32, f"w4_raw{b}")
+            src = w4_words[:, :, 1024 * b : 1024 * (b + 1)].rearrange("a p c -> p a c")
+            nc.sync.dma_start(w4_raw[b][:], src.bitcast(I32))
+
+        def load_site(s):
+            site_sb[s] = kept([P, S], F32, f"site{s}")
+            nc.sync.dma_start(site_sb[s][:], slice_rows(site, s))
+
+        def load_page(s):
+            page[s] = kept([P, T2], F32, f"page{s}")
+            nc.sync.dma_start(page[s][:], slice_rows(page0, s))
+
+        nc.sync.dma_start(list1[:], offs)
+        nc.sync.dma_start(wgs_nat[:], wgs)
+        load_tab(0)
+        for q in range(4):
+            src = tab_scales[:, 4 * q : 4 * q + 4, :].rearrange("a r t -> r a t")
+            nc.gpsimd.dma_start(tab_sc[32 * q : 32 * q + 4].bitcast(I32), src.bitcast(I32))
+        load_w1(0, 0)
+        for q in range(4):
+            src = w4_scales[:, 4 * q : 4 * q + 4, :].rearrange("a r t -> r a t")
+            nc.gpsimd.dma_start(w4_sc_raw[32 * q : 32 * q + 4].bitcast(I32), src.bitcast(I32))
+        load_tab(1)
+        load_w1(1, 0)
+        load_tab(2)
+        load_w4(0)
+        load_site(0)
+        nc.sync.dma_start(list2[:], offs2)
+        load_w1(2, 0)
+        load_page(0)
+        nc.sync.dma_start(list3[:], offs3)
+        nc.sync.dma_start(
+            vec_rows[0:4, :].rearrange("t (n i) -> t n i", i=8), tvec.rearrange("(n t i) -> t n i", t=4, i=8)
+        )
+        nc.sync.dma_start(vec_rows[4:12, 0:P], slot.rearrange("(s p) -> s p", p=P))
+
+        wgs_T = bank("e", "wgs_T")
+        for c in range(4):
+            nc.tensor.transpose(wgs_T[:, P * c : P * (c + 1)], wgs_nat[:, P * c : P * (c + 1)], ident[:])
+        wgs_sb = {}
+        for t in range(4):
+            dealt = ring.tile([P, S], F32, name=f"wgs_dealt{t}", tag="xf", bufs=4)
+            src = wgs_T[:].rearrange("p (c g t i) -> p t c g i", c=4, g=4, t=4)[:, t]
+            nc.scalar.copy(
+                dealt[:].rearrange("p (c q g i) -> p c q g i", c=4, q=4, g=4),
+                src.unsqueeze(2).to_broadcast([P, 4, 4, 4, 8]),
+            )
+            back = bank("e", f"wgs_back{t}")
+            for c in range(4):
+                nc.tensor.transpose(back[:, P * c : P * (c + 1)], dealt[:, P * c : P * (c + 1)], ident[:])
+            wgs_sb[t] = kept([P, S], F32, f"wgs_sb{t}")
+            nc.scalar.copy(wgs_sb[t][:], back[:])
+
+        v_w, v_sc = {}, {}
+
+        def gather_table(a):
+            v_w[a] = kept([P, S], U32, f"v_w{a}")
+            nc.vector.tensor_copy(v_w[a][:], tab_w[a][:].bitcast(U32).indirect(list1[:]))
+            v_sc[a] = kept([P, S], U8, f"v_sc{a}")
+            nc.vector.tensor_copy(v_sc[a][:], tab_sc[:, a, :].indirect(list1[:]))
+
+        w1_bf, w1_q, w1_sc = {}, {}, {}
+
+        def cast_w1(a, b, t, engine_copy):
+            if t == 0:
+                w1_bf[a, b] = ring.tile([P, 4, 512], BF16, name=f"w1_bf{a}{b}", tag="w1_bf", align_bytes=64)
+                w1_q[a, b] = kept([P, 512], U32, f"w1_q{a}{b}")
+                w1_sc[a, b] = kept([P, 512], U8, f"w1_sc{a}{b}")
+            engine_copy(
+                w1_bf[a, b][:, t, :].rearrange("p (g h l j) -> p g h j l", h=2, l=4, j=4),
+                w1_raw[a, b][:].rearrange("p j (g t h l) -> p t g h j l", t=4, h=2, l=4)[:, t],
+            )
+
+        def quant_w1(a, b, t0, t1):
+            cols = slice(P * t0, P * t1)
+            nc.vector.quantize_mx(
+                out=w1_q[a, b][:, cols].bitcast(E4M3X4),
+                scales=w1_sc[a, b][:, cols],
+                in_=w1_bf[a, b][:, t0:t1, :].rearrange("p t c -> p (t c)"),
+            )
+
+        w4_w = {}
+
+        def deal_w4(b):
+            w4_w[b] = kept([P, KP, 1024], U8, f"w4_w{b}")
+            nc.vector.tensor_copy(
+                w4_w[b][:].bitcast(I32).rearrange("p a (t g w) -> p a t g w", t=4, w=4),
+                w4_raw[b][:].rearrange("p a (g t w) -> p a t g w", t=4, w=4),
+            )
+
+        w4_sc = kept([P, KP * RP, 512], U8, "w4_sc")
+        for a in range(KP):
+            gather_table(a)
+            if a < KP - 1:
+                for t in range(4):
+                    cast_w1(a, 0, t, nc.scalar.copy)
+                quant_w1(a, 0, 0, 4)
+        nc.vector.tensor_copy(
+            w4_sc[:].bitcast(I32).rearrange("p n (t g w) -> p n t g w", t=4, w=2),
+            w4_sc_raw[:].bitcast(I32).rearrange("p a (b g t w) -> p (a b) t g w", b=RP, t=4, w=2),
+        )
+        deal_w4(0)
+
+        gate, gated, h_sb, picked, a_ps = {}, {}, {}, {}, {}
+
+        def gate_of(s):
+            b, t = divmod(s, 4)
+            acc = bank("ab", f"b_ps{s}")
+            for a in range(KP):
+                nc.tensor.matmul_mx(
+                    out=acc[:],
+                    lhsT=w4_w[b][:, a, 256 * t : 256 * (t + 1)].bitcast(E2M1X4),
+                    lhsT_scale=w4_sc[:, RP * a + b, P * t : P * (t + 1)],
+                    rhs=v_w[a][:].bitcast(E4M3X4),
+                    rhs_scale=v_sc[a][:],
+                    start=(a == 0),
+                    stop=(a == KP - 1),
+                )
+            gate[s] = ring.tile([P, S], F32, name=f"gate{s}", tag="gate", bufs=3)
+            nc.scalar.activation(gate[s][:], acc[:], ACT.Sigmoid)
+
+        def first_product(s):
+            b, t = divmod(s, 4)
+            a_ps[s] = bank("ab", f"a_ps{s}")
+            for a in range(KP):
+                nc.tensor.matmul_mx(
+                    out=a_ps[s][:],
+                    lhsT=w1_q[a, b][:, P * t : P * (t + 1)].bitcast(E4M3X4),
+                    lhsT_scale=w1_sc[a, b][:, P * t : P * (t + 1)],
+                    rhs=v_w[a][:].bitcast(E4M3X4),
+                    rhs_scale=v_sc[a][:],
+                    start=(a == 0),
+                    stop=(a == KP - 1),
+                )
+
+        def gate_site(s):
+            gated[s] = ring.tile([P, S], F32, name=f"gated{s}", tag="gated")
+            nc.vector.tensor_tensor(gated[s][:], site_sb[s][:], gate[s][:], ALU.mult)
+
+        def sum_h(s):
+            h_sb[s] = ring.tile([P, S], F32, name=f"h{s}", tag="h")
+            nc.vector.tensor_tensor(h_sb[s][:], a_ps[s][:], gated[s][:], ALU.add)
+
+        def scatter(s):
+            nc.vector.tensor_tensor(page[s][:].indirect(list2[:]), h_sb[s][:], wgs_sb[s % 4][:], ALU.mult)
+
+        def pick(s):
+            picked[s] = ring.tile([P, NT], F32, name=f"picked{s}", tag="xf", bufs=4)
+            nc.vector.tensor_copy(picked[s][:], page[s][:].indirect(list3[:]))
+
+        gate_of(0)
+        gate_site(0)
+        cast_w1(KP - 1, 0, 0, nc.vector.tensor_copy)
+        quant_w1(KP - 1, 0, 0, 1)
+        first_product(0)
+        sum_h(0)
+        for t in range(1, 4):
+            cast_w1(KP - 1, 0, t, nc.scalar.copy)
+            quant_w1(KP - 1, 0, t, t + 1)
+
+        load_site(1)
+        load_site(2)
+        load_page(1)
+        load_w4(1)
+        load_w1(0, 1)
+        load_site(3)
+        load_w1(1, 1)
+        load_page(2)
+        load_w1(2, 1)
+        for s in range(4, NS):
+            load_site(s)
+        for s in range(3, NS):
+            load_page(s)
+
+        vec_T = bank("e", "vec_T")
+        for b in range(RP):
+            nc.tensor.transpose(vec_T[:, P * b : P * (b + 1)], vec_rows[:, P * b : P * (b + 1)], ident[:])
+        vecs = kept([P, RP, 12], F32, "vecs")
+        nc.scalar.copy(vecs[:], vec_T[:, 0 : RP * P].rearrange("p (b c) -> p b c", b=RP)[:, :, 0:12])
+
+        x_flat = [kept([P, 4, NT], BF16, "x_flat0"), kept([P, 2, NT], BF16, "x_flat1")]
+        x_bf = [kept([P, NT, 4], BF16, f"x_bf{b}") for b in range(RP)]
+        x_q = [kept([P, NT], U32, f"x_q{b}") for b in range(RP)]
+        x_sc = [kept([P, NT], U8, f"x_sc{b}") for b in range(RP)]
+        nch = T2 // CH
+        pg_bf = {(b, c): kept([P, CH, 4], BF16, f"pg_bf{b}{c}") for b in range(RP) for c in range(nch)}
+        pg_q = {(b, c): kept([P, CH], U32, f"pg_q{b}{c}") for b in range(RP) for c in range(nch)}
+        pg_sc = {(b, c): kept([P, CH], U8, f"pg_sc{b}{c}") for b in range(RP) for c in range(nch)}
+        stage = {}
+
+        def weave(copy, dst, src, planes):
+            copy(
+                dst[:, :, 0:planes].rearrange("p (c i) t -> p c t i", i=4),
+                src.rearrange("p t (c i) -> p c t i", i=4),
+            )
+
+        def quant_x(b):
+            nc.vector.quantize_mx(
+                out=x_q[b][:].bitcast(E4M3X4), scales=x_sc[b][:], in_=x_bf[b][:].rearrange("p n t -> p (n t)")
+            )
+
+        def quant_page(b, c):
+            nc.vector.quantize_mx(
+                out=pg_q[b, c][:].bitcast(E4M3X4), scales=pg_sc[b, c][:], in_=pg_bf[b, c][:].rearrange("p n t -> p (n t)")
+            )
+
+        def templates(s):
+            b, t = divmod(s, 4)
+            mag = ring.tile([P, NT], F32, name=f"mag{s}", tag="xf", bufs=4)
+            nc.scalar.activation(mag[:], picked[s][:], ACT.Abs)
+            if s < NS - 2:
+                nc.scalar.activation(x_flat[b][:, t, :], mag[:], ACT.Copy, scale=vecs[:, b, t : t + 1])
+            else:
+                nc.vector.tensor_scalar(x_bf[b][:, :, t], mag[:], vecs[:, b, t : t + 1], None, ALU.mult)
+            if s == 3:
+                weave(nc.scalar.copy, x_bf[0], x_flat[0][:], 4)
+            if s == 5:
+                weave(nc.scalar.copy, x_bf[1], x_flat[1][:], 2)
+
+        def page_bf16(s):
+            b, t = divmod(s, 4)
+            if s < NS - 2:
+                planes = 4 if b == 0 else 2
+                if t == 0:
+                    stage[b] = big_tile([P, planes, T2], BF16, f"pg_flat{b}")
+                nc.scalar.copy(stage[b][:, t, :], page[s][:])
+                if t == planes - 1:
+                    for c in range(nch):
+                        weave(nc.scalar.copy, pg_bf[b, c], stage[b][:, :, CH * c : CH * (c + 1)], planes)
+            else:
+                for c in range(nch):
+                    nc.scalar.copy(pg_bf[1, c][:, :, t], page[s][:, CH * c : CH * (c + 1)])
+
+        e_ps = {}
+
+        def score_pass(m, b, start, stop):
+            c, u = divmod(m, CH // P)
+            nc.tensor.matmul_mx(
+                out=e_ps[m][:],
+                lhsT=pg_q[b, c][:, P * u : P * (u + 1)].bitcast(E4M3X4),
+                lhsT_scale=pg_sc[b, c][:, P * u : P * (u + 1)],
+                rhs=x_q[b][:].bitcast(E4M3X4),
+                rhs_scale=x_sc[b][:],
+                start=start,
+                stop=stop,
+            )
+
+        gate_of(1)
+        first_product(1)
+        gate_site(1)
+        for s in range(NS):
+            scatter(s)
+            if s + 1 < NS:
+                sum_h(s + 1)
+            if s + 2 < NS:
+                gate_of(s + 2)
+                first_product(s + 2)
+            if s == NS - 1:
+                nc.scalar.copy(pg_bf[1, 0][:, :, 3], page[s][:, 0:CH])
+            pick(s)
+            if s + 2 < NS:
+                gate_site(s + 2)
+            templates(s)
+            if s == NS - 1:
+                for c in range(1, nch):
+                    nc.scalar.copy(pg_bf[1, c][:, :, 3], page[s][:, CH * c : CH * (c + 1)])
+            else:
+                page_bf16(s)
+            if s < 2:
+                for a in range(KP):
+                    if (a < 2) == (s == 0):
+                        for t in range(4):
+                            cast_w1(a, 1, t, nc.scalar.copy)
+                        quant_w1(a, 1, 0, 4)
+                if s == 1:
+                    deal_w4(1)
+            if s == 5:
+                warm = kept([P, 1], F32, "warm")
+                nc.scalar.activation(warm[:], gate[NS - 1][:, 0:1], ACT.Abs_reciprocal_sqrt)
+                quant_x(0)
+                for c in range(nch):
+                    quant_page(0, c)
+                for m in range(4):
+                    e_ps[m] = bank("e", f"e_ps{m}")
+                    score_pass(m, 0, True, False)
+
+        quant_x(1)
+        for m in range(T2 // P):
+            if m % 2 == 0:
+                quant_page(1, m // 2)
+            if m < 4:
+                score_pass(m, 1, False, True)
+            else:
+                e_ps[m] = bank("ab", f"e_ps{m}")
+                score_pass(m, 1, True, False)
+                score_pass(m, 0, False, True)
+            ep = big_tile([P, 4, NT], F32, f"ep{m}")
+            parts = 2 if m == T2 // P - 1 else 1
+            for u in range(parts):
+                cols = slice(u * NT // parts, (u + 1) * NT // parts)
+                nc.scalar.activation(ep[:, 0, cols], e_ps[m][:, cols], ACT.Abs)
+                nc.scalar.activation(
+                    ep[:, 1, cols], ep[:, 0, cols], ACT.Abs_reciprocal_sqrt, bias=vecs[:, 0, 4 + m : 5 + m]
+                )
+                if m < 6:
+                    nc.gpsimd.tensor_tensor(ep[:, 2, cols], ep[:, 1, cols], ep[:, 1, cols], ALU.mult)
+                    nc.vector.tensor_tensor(ep[:, 3, cols], e_ps[m][:, cols], ep[:, 2, cols], ALU.mult)
+                else:
+                    nc.vector.tensor_tensor(ep[:, 2, cols], e_ps[m][:, cols], ep[:, 1, cols], ALU.mult)
+                    nc.vector.tensor_tensor(ep[:, 3, cols], ep[:, 2, cols], ep[:, 1, cols], ALU.mult)
+                nc.sync.dma_start(out[P * m : P * (m + 1), cols], ep[:, 3, cols])

@@ -22,6 +22,9 @@ KP = K // 512
 RP = H // 512
 NS = 4 * RP
 CH = 256
+GFROM = 8
+VABS = ()
+GSQ = ()
 
 
 def tile_list_triage_template_scores_kernel(
@@ -30,15 +33,18 @@ def tile_list_triage_template_scores_kernel(
     nc = tc.nc
     with ExitStack() as ctx:
         keep = ctx.enter_context(tc.tile_pool(name="keep", bufs=1))
-        big = ctx.enter_context(tc.tile_pool(name="big", bufs=6))
+        big = ctx.enter_context(tc.tile_pool(name="big", bufs=1))
         ring = ctx.enter_context(tc.tile_pool(name="ring", bufs=2))
         psum = ctx.enter_context(tc.psum_pool(name="psum", bufs=4))
 
         def kept(shape, dtype, name):
             return keep.tile(shape, dtype, name=name, align_bytes=64)
 
-        def big_tile(shape, dtype, name):
-            return big.tile(shape, dtype, name=name, tag="big", align_bytes=64)
+        def after(tenant, shape, dtype, name):
+            return keep.tile(shape, dtype, name=name, tag=tenant, align_bytes=64)
+
+        def big_tile(shape, dtype, name, place):
+            return big.tile(shape, dtype, name=name, tag=f"place{place}", align_bytes=64)
 
         def bank(tag, name):
             return psum.tile([P, 512], F32, name=name, tag=tag)
@@ -54,20 +60,22 @@ def tile_list_triage_template_scores_kernel(
         w4_sc_raw = kept([P, KP, H], U8, "w4_sc_raw")
         vec_rows = kept([P, 2 * P], F32, "vec_rows")
         ident = kept([P, P], F32, "ident")
-        wgs_nat = kept([P, S], F32, "wgs_nat")
+        wgs_nat = ring.tile([P, S], F32, name="wgs_nat", tag="h")
         nc.vector.memset(tab_sc[:].rearrange("p a t -> p (a t)").bitcast(I32), 0)
         nc.vector.memset(w4_sc_raw[:].rearrange("p a t -> p (a t)").bitcast(I32), 0)
         nc.vector.memset(vec_rows[:], 0.0)
         make_identity(nc, ident[:])
+        warm0 = kept([P, 1], F32, "warm0")
+        nc.scalar.activation(warm0[:], vec_rows[:, 0:1], ACT.Sigmoid)
 
         tab_w, w1_raw, w4_raw, site_sb, page = {}, {}, {}, {}, {}
 
         def load_tab(a):
-            tab_w[a] = big_tile([P, T], I32, f"tab_w{a}")
+            tab_w[a] = big_tile([P, T], I32, f"tab_w{a}", a)
             nc.sync.dma_start(tab_w[a][:], tab_words[a].rearrange("p t i -> p (t i)").bitcast(I32))
 
         def load_w1(a, b):
-            w1_raw[a, b] = big_tile([P, 4, 512], F32, f"w1_raw{a}{b}")
+            w1_raw[a, b] = big_tile([P, 4, 512], F32, f"w1_raw{a}{b}", a + KP * (1 - b))
             src = w1[512 * a : 512 * (a + 1), 512 * b : 512 * (b + 1)]
             nc.sync.dma_start(w1_raw[a, b][:], src.rearrange("(p j) c -> p j c", j=4))
 
@@ -77,7 +85,7 @@ def tile_list_triage_template_scores_kernel(
             nc.sync.dma_start(w4_raw[b][:], src.bitcast(I32))
 
         def load_site(s):
-            site_sb[s] = kept([P, S], F32, f"site{s}")
+            site_sb[s] = after(f"site{s}", [P, S], F32, f"site{s}")
             nc.sync.dma_start(site_sb[s][:], slice_rows(site, s))
 
         def load_page(s):
@@ -89,31 +97,32 @@ def tile_list_triage_template_scores_kernel(
         load_tab(0)
         for q in range(4):
             src = tab_scales[:, 4 * q : 4 * q + 4, :].rearrange("a r t -> r a t")
-            nc.gpsimd.dma_start(tab_sc[32 * q : 32 * q + 4].bitcast(I32), src.bitcast(I32))
+            nc.sync.dma_start(tab_sc[32 * q : 32 * q + 4].bitcast(I32), src.bitcast(I32))
         load_w1(0, 0)
+        load_w4(0)
+        load_tab(1)
         for q in range(4):
             src = w4_scales[:, 4 * q : 4 * q + 4, :].rearrange("a r t -> r a t")
-            nc.gpsimd.dma_start(w4_sc_raw[32 * q : 32 * q + 4].bitcast(I32), src.bitcast(I32))
-        load_tab(1)
-        load_w1(1, 0)
+            nc.sync.dma_start(w4_sc_raw[32 * q : 32 * q + 4].bitcast(I32), src.bitcast(I32))
         load_tab(2)
-        load_w4(0)
+        load_w1(1, 0)
         load_site(0)
         nc.sync.dma_start(list2[:], offs2)
         load_w1(2, 0)
-        load_page(0)
-        nc.sync.dma_start(list3[:], offs3)
         nc.sync.dma_start(
             vec_rows[0:4, :].rearrange("t (n i) -> t n i", i=8), tvec.rearrange("(n t i) -> t n i", t=4, i=8)
         )
         nc.sync.dma_start(vec_rows[4:12, 0:P], slot.rearrange("(s p) -> s p", p=P))
+        load_w4(1)
+        load_page(0)
+        nc.sync.dma_start(list3[:], offs3)
 
         wgs_T = bank("e", "wgs_T")
         for c in range(4):
             nc.tensor.transpose(wgs_T[:, P * c : P * (c + 1)], wgs_nat[:, P * c : P * (c + 1)], ident[:])
         wgs_sb = {}
         for t in range(4):
-            dealt = ring.tile([P, S], F32, name=f"wgs_dealt{t}", tag="xf", bufs=4)
+            dealt = after(f"gate{4 + t}", [P, S], F32, f"wgs_dealt{t}")
             src = wgs_T[:].rearrange("p (c g t i) -> p t c g i", c=4, g=4, t=4)[:, t]
             nc.scalar.copy(
                 dealt[:].rearrange("p (c q g i) -> p c q g i", c=4, q=4, g=4),
@@ -167,7 +176,7 @@ def tile_list_triage_template_scores_kernel(
             gather_table(a)
             if a < KP - 1:
                 for t in range(4):
-                    cast_w1(a, 0, t, nc.scalar.copy)
+                    cast_w1(a, 0, t, nc.scalar.copy if a == 0 else nc.vector.tensor_copy)
                 quant_w1(a, 0, 0, 4)
         nc.vector.tensor_copy(
             w4_sc[:].bitcast(I32).rearrange("p n (t g w) -> p n t g w", t=4, w=2),
@@ -179,7 +188,7 @@ def tile_list_triage_template_scores_kernel(
 
         def gate_of(s):
             b, t = divmod(s, 4)
-            acc = bank("ab", f"b_ps{s}")
+            acc = bank("e", f"b_ps{s}")
             for a in range(KP):
                 nc.tensor.matmul_mx(
                     out=acc[:],
@@ -190,7 +199,7 @@ def tile_list_triage_template_scores_kernel(
                     start=(a == 0),
                     stop=(a == KP - 1),
                 )
-            gate[s] = ring.tile([P, S], F32, name=f"gate{s}", tag="gate", bufs=3)
+            gate[s] = after(f"gate{s}", [P, S], F32, f"gate{s}")
             nc.scalar.activation(gate[s][:], acc[:], ACT.Sigmoid)
 
         def first_product(s):
@@ -208,18 +217,21 @@ def tile_list_triage_template_scores_kernel(
                 )
 
         def gate_site(s):
-            gated[s] = ring.tile([P, S], F32, name=f"gated{s}", tag="gated")
-            nc.vector.tensor_tensor(gated[s][:], site_sb[s][:], gate[s][:], ALU.mult)
+            engine = nc.vector if s < GFROM else nc.gpsimd
+            engine.tensor_tensor(gate[s][:], site_sb[s][:], gate[s][:], ALU.mult)
 
         def sum_h(s):
-            h_sb[s] = ring.tile([P, S], F32, name=f"h{s}", tag="h")
-            nc.vector.tensor_tensor(h_sb[s][:], a_ps[s][:], gated[s][:], ALU.add)
+            if s >= 6:
+                h_sb[s] = big_tile([P, S], F32, f"h{s}", 2)
+            else:
+                h_sb[s] = ring.tile([P, S], F32, name=f"h{s}", tag="h")
+            nc.vector.tensor_tensor(h_sb[s][:], a_ps[s][:], gate[s][:], ALU.add)
 
         def scatter(s):
             nc.vector.tensor_tensor(page[s][:].indirect(list2[:]), h_sb[s][:], wgs_sb[s % 4][:], ALU.mult)
 
         def pick(s):
-            picked[s] = ring.tile([P, NT], F32, name=f"picked{s}", tag="xf", bufs=4)
+            picked[s] = after(f"site{s}", [P, NT], F32, f"picked{s}")
             nc.vector.tensor_copy(picked[s][:], page[s][:].indirect(list3[:]))
 
         gate_of(0)
@@ -230,29 +242,23 @@ def tile_list_triage_template_scores_kernel(
         sum_h(0)
         for t in range(1, 4):
             cast_w1(KP - 1, 0, t, nc.scalar.copy)
-            quant_w1(KP - 1, 0, t, t + 1)
+        quant_w1(KP - 1, 0, 1, 2)
+        quant_w1(KP - 1, 0, 2, 4)
 
         load_site(1)
         load_site(2)
-        load_page(1)
-        load_w4(1)
         load_w1(0, 1)
-        load_site(3)
+        load_page(1)
         load_w1(1, 1)
-        load_page(2)
         load_w1(2, 1)
-        for s in range(4, NS):
-            load_site(s)
+        load_site(3)
+        load_page(2)
         for s in range(3, NS):
+            if s + 1 < NS:
+                load_site(s + 1)
             load_page(s)
 
-        vec_T = bank("e", "vec_T")
-        for b in range(RP):
-            nc.tensor.transpose(vec_T[:, P * b : P * (b + 1)], vec_rows[:, P * b : P * (b + 1)], ident[:])
-        vecs = kept([P, RP, 12], F32, "vecs")
-        nc.scalar.copy(vecs[:], vec_T[:, 0 : RP * P].rearrange("p (b c) -> p b c", b=RP)[:, :, 0:12])
-
-        x_flat = [kept([P, 4, NT], BF16, "x_flat0"), kept([P, 2, NT], BF16, "x_flat1")]
+        x_flat = [kept([P, 4, NT], BF16, "x_flat0"), kept([P, 4, NT], BF16, "x_flat1")]
         x_bf = [kept([P, NT, 4], BF16, f"x_bf{b}") for b in range(RP)]
         x_q = [kept([P, NT], U32, f"x_q{b}") for b in range(RP)]
         x_sc = [kept([P, NT], U8, f"x_sc{b}") for b in range(RP)]
@@ -262,9 +268,9 @@ def tile_list_triage_template_scores_kernel(
         pg_sc = {(b, c): kept([P, CH], U8, f"pg_sc{b}{c}") for b in range(RP) for c in range(nch)}
         stage = {}
 
-        def weave(copy, dst, src, planes):
+        def weave(copy, dst, src, t0, t1):
             copy(
-                dst[:, :, 0:planes].rearrange("p (c i) t -> p c t i", i=4),
+                dst[:, :, t0:t1].rearrange("p (c i) t -> p c t i", i=4),
                 src.rearrange("p t (c i) -> p c t i", i=4),
             )
 
@@ -280,27 +286,28 @@ def tile_list_triage_template_scores_kernel(
 
         def templates(s):
             b, t = divmod(s, 4)
-            mag = ring.tile([P, NT], F32, name=f"mag{s}", tag="xf", bufs=4)
+            mag = big_tile([P, NT], F32, f"mag{s}", 1)
             nc.scalar.activation(mag[:], picked[s][:], ACT.Abs)
-            if s < NS - 2:
+            if s < NS - 1:
                 nc.scalar.activation(x_flat[b][:, t, :], mag[:], ACT.Copy, scale=vecs[:, b, t : t + 1])
             else:
-                nc.vector.tensor_scalar(x_bf[b][:, :, t], mag[:], vecs[:, b, t : t + 1], None, ALU.mult)
+                nc.vector.tensor_scalar(x_flat[b][:, t, :], mag[:], vecs[:, b, t : t + 1], None, ALU.mult)
+                weave(nc.vector.tensor_copy, x_bf[1], x_flat[1][:, 2:4, :], 2, 4)
             if s == 3:
-                weave(nc.scalar.copy, x_bf[0], x_flat[0][:], 4)
+                weave(nc.scalar.copy, x_bf[0], x_flat[0][:], 0, 4)
             if s == 5:
-                weave(nc.scalar.copy, x_bf[1], x_flat[1][:], 2)
+                weave(nc.scalar.copy, x_bf[1], x_flat[1][:, 0:2, :], 0, 2)
 
         def page_bf16(s):
             b, t = divmod(s, 4)
             if s < NS - 2:
                 planes = 4 if b == 0 else 2
                 if t == 0:
-                    stage[b] = big_tile([P, planes, T2], BF16, f"pg_flat{b}")
+                    stage[b] = big_tile([P, planes, T2], BF16, f"pg_flat{b}", 2 + b)
                 nc.scalar.copy(stage[b][:, t, :], page[s][:])
                 if t == planes - 1:
                     for c in range(nch):
-                        weave(nc.scalar.copy, pg_bf[b, c], stage[b][:, :, CH * c : CH * (c + 1)], planes)
+                        weave(nc.scalar.copy, pg_bf[b, c], stage[b][:, :, CH * c : CH * (c + 1)], 0, planes)
             else:
                 for c in range(nch):
                     nc.scalar.copy(pg_bf[1, c][:, :, t], page[s][:, CH * c : CH * (c + 1)])
@@ -319,20 +326,39 @@ def tile_list_triage_template_scores_kernel(
                 stop=stop,
             )
 
+        def cast_second_half(a):
+            for t in range(4):
+                cast_w1(a, 1, t, nc.scalar.copy)
+            quant_w1(a, 1, 0, 4)
+
         gate_of(1)
         first_product(1)
         gate_site(1)
+        vec_T = bank("e", "vec_T")
+        for b in range(RP):
+            nc.tensor.transpose(vec_T[:, P * b : P * (b + 1)], vec_rows[:, P * b : P * (b + 1)], ident[:])
+        vecs = kept([P, RP, 12], F32, "vecs")
+        nc.scalar.copy(vecs[:], vec_T[:, 0 : RP * P].rearrange("p (b c) -> p b c", b=RP)[:, :, 0:12])
+
+        twice = kept([P, T2 // P], F32, "twice")
+        nc.scalar.activation(twice[:], vecs[:, 0, 4:12], ACT.Copy, scale=2.0)
+        deal_w4(1)
+        for r in range(2, NS):
+            gate_of(r)
+        warm = kept([P, 1], F32, "warm")
+        nc.scalar.activation(warm[:], gate[NS - 1][:, 0:1], ACT.Abs_reciprocal_sqrt)
         for s in range(NS):
             scatter(s)
             if s + 1 < NS:
                 sum_h(s + 1)
-            if s + 2 < NS:
-                gate_of(s + 2)
-                first_product(s + 2)
             if s == NS - 1:
                 nc.scalar.copy(pg_bf[1, 0][:, :, 3], page[s][:, 0:CH])
             pick(s)
+            if s == 0:
+                for a in range(KP):
+                    cast_second_half(a)
             if s + 2 < NS:
+                first_product(s + 2)
                 gate_site(s + 2)
             templates(s)
             if s == NS - 1:
@@ -340,20 +366,11 @@ def tile_list_triage_template_scores_kernel(
                     nc.scalar.copy(pg_bf[1, c][:, :, 3], page[s][:, CH * c : CH * (c + 1)])
             else:
                 page_bf16(s)
-            if s < 2:
-                for a in range(KP):
-                    if (a < 2) == (s == 0):
-                        for t in range(4):
-                            cast_w1(a, 1, t, nc.scalar.copy)
-                        quant_w1(a, 1, 0, 4)
-                if s == 1:
-                    deal_w4(1)
-            if s == 5:
-                warm = kept([P, 1], F32, "warm")
-                nc.scalar.activation(warm[:], gate[NS - 1][:, 0:1], ACT.Abs_reciprocal_sqrt)
+            if s == 4:
                 quant_x(0)
                 for c in range(nch):
                     quant_page(0, c)
+            if s == 5:
                 for m in range(4):
                     e_ps[m] = bank("e", f"e_ps{m}")
                     score_pass(m, 0, True, False)
@@ -368,15 +385,25 @@ def tile_list_triage_template_scores_kernel(
                 e_ps[m] = bank("ab", f"e_ps{m}")
                 score_pass(m, 1, True, False)
                 score_pass(m, 0, False, True)
-            ep = big_tile([P, 4, NT], F32, f"ep{m}")
+            ep = big_tile([P, 4, NT], F32, f"ep{m}", (4 + m) % 6)
             parts = 2 if m == T2 // P - 1 else 1
             for u in range(parts):
                 cols = slice(u * NT // parts, (u + 1) * NT // parts)
-                nc.scalar.activation(ep[:, 0, cols], e_ps[m][:, cols], ACT.Abs)
-                nc.scalar.activation(
-                    ep[:, 1, cols], ep[:, 0, cols], ACT.Abs_reciprocal_sqrt, bias=vecs[:, 0, 4 + m : 5 + m]
-                )
-                if m < 6:
+                soft = vecs[:, 0, 4 + m : 5 + m]
+                if m in VABS:
+                    nc.vector.tensor_scalar(
+                        ep[:, 2, cols], e_ps[m][:, cols], 0.0, twice[:, m : m + 1], ALU.is_ge, ALU.mult
+                    )
+                    nc.vector.scalar_tensor_tensor(
+                        ep[:, 0, cols], e_ps[m][:, cols], soft, ep[:, 2, cols], ALU.subtract, ALU.add
+                    )
+                    nc.scalar.activation(ep[:, 1, cols], ep[:, 0, cols], ACT.Abs_reciprocal_sqrt)
+                else:
+                    nc.scalar.activation(ep[:, 0, cols], e_ps[m][:, cols], ACT.Abs)
+                    nc.scalar.activation(ep[:, 1, cols], ep[:, 0, cols], ACT.Abs_reciprocal_sqrt, bias=soft)
+            for u in range(parts):
+                cols = slice(u * NT // parts, (u + 1) * NT // parts)
+                if m in GSQ:
                     nc.gpsimd.tensor_tensor(ep[:, 2, cols], ep[:, 1, cols], ep[:, 1, cols], ALU.mult)
                     nc.vector.tensor_tensor(ep[:, 3, cols], e_ps[m][:, cols], ep[:, 2, cols], ALU.mult)
                 else:

@@ -20,11 +20,20 @@ ALU = mybir.AluOpType
 P = 128
 KP = K // 512
 RP = H // 512
-NS = 4 * RP
-CH = 256
-GFROM = 8
-VABS = ()
-GSQ = ()
+NS = H // P
+MB = T2 // P
+JB = NT // P
+W1_CHUNKS = ((0, 1), (1, 2), (2, 4), (4, 6), (6, 8))
+VCAST = -1 + 1
+FIRST = 1
+BFB = 4
+EM = 0
+ET = "..atgatg"
+GB = 1
+HG = 3
+H_OWN = {HG: "bf_last"}
+H_AFTER = ("h0", "h1", "h0", "h1", "h0", "h1", "woven6", "woven7")
+BF_AFTER = ("b0", "b1", "b0", "b1", "b0", "b1", "b0", "b1")
 
 
 def tile_list_triage_template_scores_kernel(
@@ -35,7 +44,7 @@ def tile_list_triage_template_scores_kernel(
         keep = ctx.enter_context(tc.tile_pool(name="keep", bufs=1))
         big = ctx.enter_context(tc.tile_pool(name="big", bufs=1))
         ring = ctx.enter_context(tc.tile_pool(name="ring", bufs=2))
-        psum = ctx.enter_context(tc.psum_pool(name="psum", bufs=4))
+        psum = ctx.enter_context(tc.psum_pool(name="psum", bufs=2))
 
         def kept(shape, dtype, name):
             return keep.tile(shape, dtype, name=name, align_bytes=64)
@@ -46,93 +55,83 @@ def tile_list_triage_template_scores_kernel(
         def big_tile(shape, dtype, name, place):
             return big.tile(shape, dtype, name=name, tag=f"place{place}", align_bytes=64)
 
-        def bank(tag, name):
-            return psum.tile([P, 512], F32, name=name, tag=tag)
+        def ringed(shape, dtype, name, tag, bufs):
+            return ring.tile(shape, dtype, name=name, tag=tag, bufs=bufs, align_bytes=64)
 
-        def slice_rows(src, s):
-            b, t = divmod(s, 4)
-            return src.rearrange("(b g t i) m -> b t g i m", b=RP, t=4, i=8)[b, t]
+        def bank(tag, name):
+            return psum.tile([P, 512], F32, name=name, tag=tag)[:]
+
+        def two_banks(name):
+            both = psum.tile([P, 2, 512], F32, name=name, tag="double", bufs=1)
+            return both[:, 0, :], both[:, 1, :]
 
         list1 = keep.tile([P, S // 16], U16, name="list1")
         list2 = keep.tile([P, S // 16], U16, name="list2")
         list3 = keep.tile([P, NT // 16], U16, name="list3")
         tab_sc = kept([P, KP, T], U8, "tab_sc")
-        w4_sc_raw = kept([P, KP, H], U8, "w4_sc_raw")
-        vec_rows = kept([P, 2 * P], F32, "vec_rows")
+        w4_sc = kept([P, KP, H], U8, "w4_sc")
+        vec_rows = after("mx0", [P, P], F32, "vec_rows")
         ident = kept([P, P], F32, "ident")
-        wgs_nat = ring.tile([P, S], F32, name="wgs_nat", tag="h")
+        ident_bf = kept([P, P], BF16, "ident_bf")
+        wgs_sb = kept([P, S], F32, "wgs_sb")
         nc.vector.memset(tab_sc[:].rearrange("p a t -> p (a t)").bitcast(I32), 0)
-        nc.vector.memset(w4_sc_raw[:].rearrange("p a t -> p (a t)").bitcast(I32), 0)
+        nc.vector.memset(w4_sc[:].rearrange("p a t -> p (a t)").bitcast(I32), 0)
         nc.vector.memset(vec_rows[:], 0.0)
         make_identity(nc, ident[:])
+        make_identity(nc, ident_bf[:])
         warm0 = kept([P, 1], F32, "warm0")
-        nc.scalar.activation(warm0[:], vec_rows[:, 0:1], ACT.Sigmoid)
+        nc.scalar.activation(warm0[:], ident[:, 0:1], ACT.Sigmoid)
 
-        tab_w, w1_raw, w4_raw, site_sb, page = {}, {}, {}, {}, {}
+        tab_w, w1_raw, w4_w, site_sb, page = {}, {}, {}, {}, {}
 
         def load_tab(a):
             tab_w[a] = big_tile([P, T], I32, f"tab_w{a}", a)
             nc.sync.dma_start(tab_w[a][:], tab_words[a].rearrange("p t i -> p (t i)").bitcast(I32))
 
-        def load_w1(a, b):
-            w1_raw[a, b] = big_tile([P, 4, 512], F32, f"w1_raw{a}{b}", a + KP * (1 - b))
-            src = w1[512 * a : 512 * (a + 1), 512 * b : 512 * (b + 1)]
-            nc.sync.dma_start(w1_raw[a, b][:], src.rearrange("(p j) c -> p j c", j=4))
+        def load_scales(dst, src):
+            for q in range(4):
+                rows = src[:, 4 * q : 4 * q + 4, :].rearrange("a r t -> r a t")
+                nc.sync.dma_start(dst[32 * q : 32 * q + 4].bitcast(I32), rows.bitcast(I32))
+
+        def load_w1(chunk, a):
+            s0, s1 = W1_CHUNKS[chunk]
+            place = a if chunk == 3 else f"{chunk}{a}"
+            raw = big_tile([P, 4, P * (s1 - s0)], F32, f"w1_raw{chunk}{a}", place)
+            src = w1[512 * a : 512 * (a + 1), P * s0 : P * s1]
+            nc.sync.dma_start(raw[:], src.rearrange("(p j) c -> p j c", j=4))
+            for s in range(s0, s1):
+                w1_raw[s, a] = raw[:, :, P * (s - s0) : P * (s - s0 + 1)]
 
         def load_w4(b):
-            w4_raw[b] = kept([P, KP, 256], I32, f"w4_raw{b}")
+            w4_w[b] = kept([P, KP, 1024], U8, f"w4_w{b}")
             src = w4_words[:, :, 1024 * b : 1024 * (b + 1)].rearrange("a p c -> p a c")
-            nc.sync.dma_start(w4_raw[b][:], src.bitcast(I32))
+            nc.sync.dma_start(w4_w[b][:].bitcast(I32), src.bitcast(I32))
 
         def load_site(s):
             site_sb[s] = after(f"site{s}", [P, S], F32, f"site{s}")
-            nc.sync.dma_start(site_sb[s][:], slice_rows(site, s))
+            nc.sync.dma_start(site_sb[s][:], site[P * s : P * (s + 1), :])
 
         def load_page(s):
             page[s] = kept([P, T2], F32, f"page{s}")
-            nc.sync.dma_start(page[s][:], slice_rows(page0, s))
+            nc.sync.dma_start(page[s][:], page0[P * s : P * (s + 1), :])
 
         nc.sync.dma_start(list1[:], offs)
-        nc.sync.dma_start(wgs_nat[:], wgs)
         load_tab(0)
-        for q in range(4):
-            src = tab_scales[:, 4 * q : 4 * q + 4, :].rearrange("a r t -> r a t")
-            nc.sync.dma_start(tab_sc[32 * q : 32 * q + 4].bitcast(I32), src.bitcast(I32))
-        load_w1(0, 0)
-        load_w4(0)
+        load_scales(tab_sc, tab_scales)
         load_tab(1)
-        for q in range(4):
-            src = w4_scales[:, 4 * q : 4 * q + 4, :].rearrange("a r t -> r a t")
-            nc.sync.dma_start(w4_sc_raw[32 * q : 32 * q + 4].bitcast(I32), src.bitcast(I32))
+        load_scales(w4_sc, w4_scales)
+        load_w4(0)
         load_tab(2)
-        load_w1(1, 0)
+        for a in range(KP):
+            load_w1(0, a)
         load_site(0)
+        nc.sync.dma_start(wgs_sb[:], wgs)
         nc.sync.dma_start(list2[:], offs2)
-        load_w1(2, 0)
-        nc.sync.dma_start(
-            vec_rows[0:4, :].rearrange("t (n i) -> t n i", i=8), tvec.rearrange("(n t i) -> t n i", t=4, i=8)
-        )
-        nc.sync.dma_start(vec_rows[4:12, 0:P], slot.rearrange("(s p) -> s p", p=P))
-        load_w4(1)
         load_page(0)
+        load_w4(1)
+        for a in range(KP):
+            load_w1(1, a)
         nc.sync.dma_start(list3[:], offs3)
-
-        wgs_T = bank("e", "wgs_T")
-        for c in range(4):
-            nc.tensor.transpose(wgs_T[:, P * c : P * (c + 1)], wgs_nat[:, P * c : P * (c + 1)], ident[:])
-        wgs_sb = {}
-        for t in range(4):
-            dealt = after(f"gate{4 + t}", [P, S], F32, f"wgs_dealt{t}")
-            src = wgs_T[:].rearrange("p (c g t i) -> p t c g i", c=4, g=4, t=4)[:, t]
-            nc.scalar.copy(
-                dealt[:].rearrange("p (c q g i) -> p c q g i", c=4, q=4, g=4),
-                src.unsqueeze(2).to_broadcast([P, 4, 4, 4, 8]),
-            )
-            back = bank("e", f"wgs_back{t}")
-            for c in range(4):
-                nc.tensor.transpose(back[:, P * c : P * (c + 1)], dealt[:, P * c : P * (c + 1)], ident[:])
-            wgs_sb[t] = kept([P, S], F32, f"wgs_sb{t}")
-            nc.scalar.copy(wgs_sb[t][:], back[:])
 
         v_w, v_sc = {}, {}
 
@@ -142,58 +141,41 @@ def tile_list_triage_template_scores_kernel(
             v_sc[a] = kept([P, S], U8, f"v_sc{a}")
             nc.vector.tensor_copy(v_sc[a][:], tab_sc[:, a, :].indirect(list1[:]))
 
-        w1_bf, w1_q, w1_sc = {}, {}, {}
+        w1_q, w1_sc, bf_last = {}, {}, []
 
-        def cast_w1(a, b, t, engine_copy):
-            if t == 0:
-                w1_bf[a, b] = ring.tile([P, 4, 512], BF16, name=f"w1_bf{a}{b}", tag="w1_bf", align_bytes=64)
-                w1_q[a, b] = kept([P, 512], U32, f"w1_q{a}{b}")
-                w1_sc[a, b] = kept([P, 512], U8, f"w1_sc{a}{b}")
-            engine_copy(
-                w1_bf[a, b][:, t, :].rearrange("p (g h l j) -> p g h j l", h=2, l=4, j=4),
-                w1_raw[a, b][:].rearrange("p j (g t h l) -> p t g h j l", t=4, h=2, l=4)[:, t],
-            )
-
-        def quant_w1(a, b, t0, t1):
-            cols = slice(P * t0, P * t1)
+        def quant_w1_part(s, a0, a1):
+            copy = nc.vector.tensor_copy if s < VCAST else nc.scalar.copy
+            if s < NS - 1:
+                w1_bf = ringed([P, a1 - a0, P, 4], BF16, f"w1_bf{s}{a0}", f"w1_bf{a0}", BFB)[:]
+            else:
+                if a0 == 0:
+                    bf_last.append(after("bf_last", [P, KP, P, 4], BF16, "w1_bf_last"))
+                w1_bf = bf_last[0][:, a0:a1]
+            if a0 == 0:
+                w1_q[s] = ringed([P, KP * P], U32, f"w1_q{s}", "w1_q", 6)
+                w1_sc[s] = ringed([P, KP * P], U8, f"w1_sc{s}", "w1_sc", 6)
+            for a in range(a0, a1):
+                copy(w1_bf[:, a - a0], w1_raw[s, a].rearrange("p j c -> p c j"))
             nc.vector.quantize_mx(
-                out=w1_q[a, b][:, cols].bitcast(E4M3X4),
-                scales=w1_sc[a, b][:, cols],
-                in_=w1_bf[a, b][:, t0:t1, :].rearrange("p t c -> p (t c)"),
+                out=w1_q[s][:, P * a0 : P * a1].bitcast(E4M3X4),
+                scales=w1_sc[s][:, P * a0 : P * a1],
+                in_=w1_bf.rearrange("p a c j -> p (a c j)"),
             )
 
-        w4_w = {}
+        def quant_w1(s):
+            quant_w1_part(s, 0, 2)
+            quant_w1_part(s, 2, 3)
 
-        def deal_w4(b):
-            w4_w[b] = kept([P, KP, 1024], U8, f"w4_w{b}")
-            nc.vector.tensor_copy(
-                w4_w[b][:].bitcast(I32).rearrange("p a (t g w) -> p a t g w", t=4, w=4),
-                w4_raw[b][:].rearrange("p a (g t w) -> p a t g w", t=4, w=4),
-            )
-
-        w4_sc = kept([P, KP * RP, 512], U8, "w4_sc")
-        for a in range(KP):
-            gather_table(a)
-            if a < KP - 1:
-                for t in range(4):
-                    cast_w1(a, 0, t, nc.scalar.copy if a == 0 else nc.vector.tensor_copy)
-                quant_w1(a, 0, 0, 4)
-        nc.vector.tensor_copy(
-            w4_sc[:].bitcast(I32).rearrange("p n (t g w) -> p n t g w", t=4, w=2),
-            w4_sc_raw[:].bitcast(I32).rearrange("p a (b g t w) -> p (a b) t g w", b=RP, t=4, w=2),
-        )
-        deal_w4(0)
-
-        gate, gated, h_sb, picked, a_ps = {}, {}, {}, {}, {}
+        gate, a_ps, h_sb, picked, pair = {}, {}, {}, {}, {}
 
         def gate_of(s):
             b, t = divmod(s, 4)
-            acc = bank("e", f"b_ps{s}")
+            acc = bank("g", f"b_ps{s}")
             for a in range(KP):
                 nc.tensor.matmul_mx(
                     out=acc[:],
                     lhsT=w4_w[b][:, a, 256 * t : 256 * (t + 1)].bitcast(E2M1X4),
-                    lhsT_scale=w4_sc[:, RP * a + b, P * t : P * (t + 1)],
+                    lhsT_scale=w4_sc[:, a, P * s : P * (s + 1)],
                     rhs=v_w[a][:].bitcast(E4M3X4),
                     rhs_scale=v_sc[a][:],
                     start=(a == 0),
@@ -203,13 +185,12 @@ def tile_list_triage_template_scores_kernel(
             nc.scalar.activation(gate[s][:], acc[:], ACT.Sigmoid)
 
         def first_product(s):
-            b, t = divmod(s, 4)
-            a_ps[s] = bank("ab", f"a_ps{s}")
+            a_ps[s] = bank("a" if s % 4 < 2 else "g", f"a_ps{s}")
             for a in range(KP):
                 nc.tensor.matmul_mx(
                     out=a_ps[s][:],
-                    lhsT=w1_q[a, b][:, P * t : P * (t + 1)].bitcast(E4M3X4),
-                    lhsT_scale=w1_sc[a, b][:, P * t : P * (t + 1)],
+                    lhsT=w1_q[s][:, P * a : P * (a + 1)].bitcast(E4M3X4),
+                    lhsT_scale=w1_sc[s][:, P * a : P * (a + 1)],
                     rhs=v_w[a][:].bitcast(E4M3X4),
                     rhs_scale=v_sc[a][:],
                     start=(a == 0),
@@ -217,196 +198,232 @@ def tile_list_triage_template_scores_kernel(
                 )
 
         def gate_site(s):
-            engine = nc.vector if s < GFROM else nc.gpsimd
-            engine.tensor_tensor(gate[s][:], site_sb[s][:], gate[s][:], ALU.mult)
+            nc.vector.tensor_tensor(site_sb[s][:], site_sb[s][:], gate[s][:], ALU.mult)
 
-        def sum_h(s):
-            if s >= 6:
-                h_sb[s] = big_tile([P, S], F32, f"h{s}", 2)
-            else:
-                h_sb[s] = ring.tile([P, S], F32, name=f"h{s}", tag="h")
-            nc.vector.tensor_tensor(h_sb[s][:], a_ps[s][:], gate[s][:], ALU.add)
+        def make_h(s):
+            h_sb[s] = after(H_OWN[s], [P, S], F32, f"h{s}")[:] if s in H_OWN else site_sb[s][:]
+            nc.vector.tensor_tensor(h_sb[s], a_ps[s][:], site_sb[s][:], ALU.add)
 
         def scatter(s):
-            nc.vector.tensor_tensor(page[s][:].indirect(list2[:]), h_sb[s][:], wgs_sb[s % 4][:], ALU.mult)
+            nc.vector.tensor_tensor(page[s][:].indirect(list2[:]), h_sb[s], wgs_sb[:], ALU.mult)
 
         def pick(s):
-            picked[s] = after(f"site{s}", [P, NT], F32, f"picked{s}")
-            nc.vector.tensor_copy(picked[s][:], page[s][:].indirect(list3[:]))
+            picked[s] = after(f"gate{s}", [P, NT], F32, f"picked{s}")[:]
+            nc.vector.tensor_copy(picked[s], page[s][:].indirect(list3[:]))
 
+        for a in range(KP):
+            gather_table(a)
+            if a == 0:
+                quant_w1(0)
         gate_of(0)
-        gate_site(0)
-        cast_w1(KP - 1, 0, 0, nc.vector.tensor_copy)
-        quant_w1(KP - 1, 0, 0, 1)
         first_product(0)
-        sum_h(0)
-        for t in range(1, 4):
-            cast_w1(KP - 1, 0, t, nc.scalar.copy)
-        quant_w1(KP - 1, 0, 1, 2)
-        quant_w1(KP - 1, 0, 2, 4)
+        gate_site(0)
+        make_h(0)
 
         load_site(1)
-        load_site(2)
-        load_w1(0, 1)
+        for a in range(KP):
+            load_w1(2, a)
         load_page(1)
-        load_w1(1, 1)
-        load_w1(2, 1)
-        load_site(3)
+        load_site(2)
+        for a in range(KP):
+            load_w1(3, a)
         load_page(2)
-        for s in range(3, NS):
-            if s + 1 < NS:
-                load_site(s + 1)
-            load_page(s)
+        for a in range(KP):
+            load_w1(4, a)
+        load_site(3)
+        nc.sync.dma_start(vec_rows[0:NS, :], tvec.rearrange("(s p) -> s p", p=P))
+        nc.sync.dma_start(vec_rows[NS : NS + MB, :], slot.rearrange("(s p) -> s p", p=P))
+        load_page(3)
+        load_site(4)
+        load_page(4)
+        load_site(5)
+        load_page(5)
+        load_site(6)
+        load_page(6)
+        load_site(7)
+        load_page(7)
 
-        x_flat = [kept([P, 4, NT], BF16, "x_flat0"), kept([P, 4, NT], BF16, "x_flat1")]
-        x_bf = [kept([P, NT, 4], BF16, f"x_bf{b}") for b in range(RP)]
-        x_q = [kept([P, NT], U32, f"x_q{b}") for b in range(RP)]
+        vecs = {}
+
+
+        page_T = {(b, h): kept([P, 4, 2, P, 2], BF16, f"page_T{b}{h}") for b in range(RP) for h in range(2)}
+        x_T = {b: kept([P, JB, 2, P], F32, f"x_T{b}") for b in range(RP)}
+        x_bf, pg_bf = {}, {}
+        x_q = {1: kept([P, NT], U32, "x_q1")[:]}
         x_sc = [kept([P, NT], U8, f"x_sc{b}") for b in range(RP)]
-        nch = T2 // CH
-        pg_bf = {(b, c): kept([P, CH, 4], BF16, f"pg_bf{b}{c}") for b in range(RP) for c in range(nch)}
-        pg_q = {(b, c): kept([P, CH], U32, f"pg_q{b}{c}") for b in range(RP) for c in range(nch)}
-        pg_sc = {(b, c): kept([P, CH], U8, f"pg_sc{b}{c}") for b in range(RP) for c in range(nch)}
-        stage = {}
+        pg_q = {(1, c): kept([P, 2 * P], U32, f"pg_q1{c}")[:] for c in range(MB // 2)}
+        pg_sc = {(b, c): kept([P, 2 * P], U8, f"pg_sc{b}{c}") for b in range(RP) for c in range(MB // 2)}
 
-        def weave(copy, dst, src, t0, t1):
+        def turn_page(s, h, turned):
+            b, t = divmod(s, 4)
+            for i in range(4):
+                m0 = P * (4 * h + i)
+                nc.tensor.transpose(turned[:, P * i : P * (i + 1)], page[s][:, m0 : m0 + P], ident[:])
+            copy = nc.vector.tensor_copy if s == NS else nc.scalar.copy
             copy(
-                dst[:, :, t0:t1].rearrange("p (c i) t -> p c t i", i=4),
-                src.rearrange("p t (c i) -> p c t i", i=4),
+                page_T[b, h][:, :, :, 32 * t : 32 * (t + 1), :],
+                turned[:].rearrange("p (i q u e) -> p i u q e", i=4, u=2, e=2),
             )
 
-        def quant_x(b):
-            nc.vector.quantize_mx(
-                out=x_q[b][:].bitcast(E4M3X4), scales=x_sc[b][:], in_=x_bf[b][:].rearrange("p n t -> p (n t)")
-            )
-
-        def quant_page(b, c):
-            nc.vector.quantize_mx(
-                out=pg_q[b, c][:].bitcast(E4M3X4), scales=pg_sc[b, c][:], in_=pg_bf[b, c][:].rearrange("p n t -> p (n t)")
-            )
-
-        def templates(s):
+        def turn_x(s, between):
             b, t = divmod(s, 4)
-            mag = big_tile([P, NT], F32, f"mag{s}", 1)
-            nc.scalar.activation(mag[:], picked[s][:], ACT.Abs)
-            if s < NS - 1:
-                nc.scalar.activation(x_flat[b][:, t, :], mag[:], ACT.Copy, scale=vecs[:, b, t : t + 1])
-            else:
-                nc.vector.tensor_scalar(x_flat[b][:, t, :], mag[:], vecs[:, b, t : t + 1], None, ALU.mult)
-                weave(nc.vector.tensor_copy, x_bf[1], x_flat[1][:, 2:4, :], 2, 4)
-            if s == 3:
-                weave(nc.scalar.copy, x_bf[0], x_flat[0][:], 0, 4)
-            if s == 5:
-                weave(nc.scalar.copy, x_bf[1], x_flat[1][:, 0:2, :], 0, 2)
+            mag = after("mx0", [P, NT], F32, f"mag{s}")
+            nc.scalar.activation(mag[:], picked[s], ACT.Abs)
+            places = ("xf0", "codes0") if s == NS - 2 else (f"xf{s % 2}",)
+            width = NT // len(places)
+            x_flat = [after(place, [P, width], BF16, f"x_flat{s}{place}") for place in places]
+            for c, part in enumerate(x_flat):
+                nc.scalar.activation(part[:], mag[:, width * c : width * (c + 1)], ACT.Copy, scale=vecs[:, s : s + 1])
+            between()
+            turned = two_banks(f"x_ps{s}")[0] if s < NS - 1 else bank("a", f"x_ps{s}")
+            for i in range(JB):
+                nc.tensor.transpose(
+                    turned[:].bitcast(BF16)[:, P * i : P * (i + 1)], x_flat[P * i // width][:, P * i % width : P * i % width + P], ident_bf[:]
+                )
+            nc.scalar.copy(
+                x_T[b][:, :, :, 32 * t : 32 * (t + 1)],
+                turned[:, 0 : JB * P // 2].rearrange("p (i q u) -> p i u q", i=JB, u=2),
+            )
 
-        def page_bf16(s):
-            b, t = divmod(s, 4)
-            if s < NS - 2:
-                planes = 4 if b == 0 else 2
-                if t == 0:
-                    stage[b] = big_tile([P, planes, T2], BF16, f"pg_flat{b}", 2 + b)
-                nc.scalar.copy(stage[b][:, t, :], page[s][:])
-                if t == planes - 1:
-                    for c in range(nch):
-                        weave(nc.scalar.copy, pg_bf[b, c], stage[b][:, :, CH * c : CH * (c + 1)], 0, planes)
-            else:
-                for c in range(nch):
-                    nc.scalar.copy(pg_bf[1, c][:, :, t], page[s][:, CH * c : CH * (c + 1)])
+        def turn_back(words, tag, name, copy, place):
+            back = bank(tag, f"{name}_ps")
+            for i in range(2):
+                for u in range(2):
+                    o = P * (2 * i + u)
+                    nc.tensor.transpose(back[:, o : o + P], words[:, i, u, :], ident[:])
+            woven = after(place, [P, 2 * P * 4], BF16, f"{name}_bf")
+            copy(
+                woven[:].bitcast(F32).rearrange("p (i m u) -> p i m u", i=2, u=2),
+                back[:].rearrange("p (i u m) -> p i m u", i=2, u=2),
+            )
+            return woven
+
+        def quantise(woven, codes, scales):
+            nc.vector.quantize_mx(out=codes.bitcast(E4M3X4), scales=scales, in_=woven[:])
+
+        def quant_x(b, c, tag, copy):
+            x_bf[b, c] = turn_back(x_T[b][:, 2 * c : 2 * c + 2], tag, f"x{b}{c}", copy, f"wx{c}")
+            if b == 1:
+                quantise_x(b, c)
+
+        def quantise_x(b, c):
+            cols = slice(2 * P * c, 2 * P * (c + 1))
+            quantise(x_bf[b, c], x_q[b][:, cols], x_sc[b][:, cols])
+
+        def quant_page(b, c, tag, copy):
+            h, i = divmod(c, 2)
+            words = page_T[b, h][:].rearrange("p i u q e -> p (i u q e)").bitcast(F32)
+            words = words.rearrange("p (i u q) -> p i u q", i=4, u=2)[:, 2 * i : 2 * i + 2]
+            pg_bf[b, c] = turn_back(words, tag, f"pg{b}{c}", copy, f"wp{c}")
+            if b == 1:
+                quantise(pg_bf[b, c], pg_q[b, c], pg_sc[b, c][:])
 
         e_ps = {}
 
-        def score_pass(m, b, start, stop):
-            c, u = divmod(m, CH // P)
+        def score_pass(m, b, cols, start, stop):
+            c, i = divmod(m, 2)
             nc.tensor.matmul_mx(
-                out=e_ps[m][:],
-                lhsT=pg_q[b, c][:, P * u : P * (u + 1)].bitcast(E4M3X4),
-                lhsT_scale=pg_sc[b, c][:, P * u : P * (u + 1)],
-                rhs=x_q[b][:].bitcast(E4M3X4),
-                rhs_scale=x_sc[b][:],
+                out=e_ps[m][:, cols],
+                lhsT=pg_q[b, c][:, P * i : P * (i + 1)].bitcast(E4M3X4),
+                lhsT_scale=pg_sc[b, c][:, P * i : P * (i + 1)],
+                rhs=x_q[b][:, cols].bitcast(E4M3X4),
+                rhs_scale=x_sc[b][:, cols],
                 start=start,
                 stop=stop,
             )
 
-        def cast_second_half(a):
-            for t in range(4):
-                cast_w1(a, 1, t, nc.scalar.copy)
-            quant_w1(a, 1, 0, 4)
-
-        gate_of(1)
-        first_product(1)
-        gate_site(1)
-        vec_T = bank("e", "vec_T")
-        for b in range(RP):
-            nc.tensor.transpose(vec_T[:, P * b : P * (b + 1)], vec_rows[:, P * b : P * (b + 1)], ident[:])
-        vecs = kept([P, RP, 12], F32, "vecs")
-        nc.scalar.copy(vecs[:], vec_T[:, 0 : RP * P].rearrange("p (b c) -> p b c", b=RP)[:, :, 0:12])
-
-        twice = kept([P, T2 // P], F32, "twice")
-        nc.scalar.activation(twice[:], vecs[:, 0, 4:12], ACT.Copy, scale=2.0)
-        deal_w4(1)
-        for r in range(2, NS):
-            gate_of(r)
+        for s in range(1, NS):
+            gate_of(s)
+        for s in range(1, NS):
+            quant_w1(s)
         warm = kept([P, 1], F32, "warm")
         nc.scalar.activation(warm[:], gate[NS - 1][:, 0:1], ACT.Abs_reciprocal_sqrt)
-        for s in range(NS):
-            scatter(s)
-            if s + 1 < NS:
-                sum_h(s + 1)
-            if s == NS - 1:
-                nc.scalar.copy(pg_bf[1, 0][:, :, 3], page[s][:, 0:CH])
-            pick(s)
-            if s == 0:
-                for a in range(KP):
-                    cast_second_half(a)
-            if s + 2 < NS:
-                first_product(s + 2)
-                gate_site(s + 2)
-            templates(s)
-            if s == NS - 1:
-                for c in range(1, nch):
-                    nc.scalar.copy(pg_bf[1, c][:, :, 3], page[s][:, CH * c : CH * (c + 1)])
-            else:
-                page_bf16(s)
+        for s in range(1, NS):
+            first_product(s)
+            gate_site(s)
+            make_h(s)
+            scatter(s - 1)
+            pick(s - 1)
+        scatter(NS - 1)
+        vecs = after(f"site{HG}", [P, NS + MB], F32, "vecs")
+        for c0, c1 in ((0, NS), (NS, NS + MB)):
+            vec_T = bank("t", f"vec_T{c0}")
+            nc.tensor.transpose(vec_T[:, 0:P], vec_rows[:], ident[:])
+            nc.scalar.copy(vecs[:, c0:c1], vec_T[:, c0:c1])
+        for s in range(NS - 1):
             if s == 4:
-                quant_x(0)
-                for c in range(nch):
-                    quant_page(0, c)
-            if s == 5:
-                for m in range(4):
-                    e_ps[m] = bank("e", f"e_ps{m}")
-                    score_pass(m, 0, True, False)
+                for c in range(MB // 2):
+                    quant_page(0, c, "a", nc.scalar.copy)
+                for c in range(2):
+                    quant_x(0, c, "a", nc.scalar.copy)
+            banks = (bank("t", f"page_ps{s}0"), bank("t", f"page_ps{s}1"))
+            turn_page(s, 0, banks[0])
+            turn_x(s, lambda: turn_page(s, 1, banks[1]))
 
-        quant_x(1)
-        for m in range(T2 // P):
+        last = NS - 1
+        half = NT // 2
+        picked_last = after("xf0", [P, NT], F32, "picked_last")
+        mag_last = after("mx0", [P, NT], F32, "mag_last")
+        x_last = after("xf1", [P, NT], BF16, "x_last")
+        banks = two_banks("last_ps")
+        for c in range(2):
+            cols = slice(half * c, half * (c + 1))
+            offsets = list3[:, half // 16 * c : half // 16 * (c + 1)]
+            nc.vector.tensor_copy(picked_last[:, cols], page[last][:].indirect(offsets))
+            nc.scalar.activation(mag_last[:, cols], picked_last[:, cols], ACT.Abs)
+        for c in range(2):
+            cols = slice(half * c, half * (c + 1))
+            nc.vector.tensor_scalar(x_last[:, cols], mag_last[:, cols], vecs[:, last : last + 1], None, ALU.mult)
+            turned = bank("a", f"x_last_ps{c}")
+            for i in range(2):
+                j0 = half * c + P * i
+                nc.tensor.transpose(turned.bitcast(BF16)[:, P * i : P * (i + 1)], x_last[:, j0 : j0 + P], ident_bf[:])
+            nc.vector.tensor_copy(
+                x_T[1][:, 2 * c : 2 * c + 2, :, 96:128],
+                turned[:, 0:P].rearrange("p (i q u) -> p i u q", i=2, u=2),
+            )
+        turn_page(last, 0, banks[0])
+        turn_page(last, 1, banks[1])
+        codes0 = after("codes0", [P, NT + T2], U32, "codes0")
+        x_q[0] = codes0[:, 0:NT]
+        for c in range(MB // 2):
+            pg_q[0, c] = codes0[:, NT + 2 * P * c : NT + 2 * P * (c + 1)]
+        for c in range(2):
+            quantise_x(0, c)
+        for c in range(MB // 2):
+            quantise(pg_bf[0, c], pg_q[0, c], pg_sc[0, c][:])
+        quant_x(1, 0, "g", nc.vector.tensor_copy)
+        quant_page(1, 0, "t", nc.scalar.copy)
+        quant_x(1, 1, "g", nc.scalar.copy)
+        quant_page(1, 1, "t", nc.vector.tensor_copy)
+        quant_page(1, 2, "a", nc.scalar.copy)
+        quant_page(1, 3, "a", nc.scalar.copy)
+        for m in range(MB):
+            if m == EM:
+                e_ps[m], e_ps[m + 1] = two_banks("e_pair")
+            elif m != EM + 1:
+                e_ps[m] = bank(ET[m], f"e_ps{m}")
+            groups = 2 if m == 0 else 1
+            for u in range(groups):
+                cols = slice(u * NT // groups, (u + 1) * NT // groups)
+                score_pass(m, FIRST, cols, True, False)
+                score_pass(m, 1 - FIRST, cols, False, True)
             if m % 2 == 0:
-                quant_page(1, m // 2)
-            if m < 4:
-                score_pass(m, 1, False, True)
-            else:
-                e_ps[m] = bank("ab", f"e_ps{m}")
-                score_pass(m, 1, True, False)
-                score_pass(m, 0, False, True)
-            ep = big_tile([P, 4, NT], F32, f"ep{m}", (4 + m) % 6)
-            parts = 2 if m == T2 // P - 1 else 1
+                ep_pair = big_tile([P, 2, 2, NT], F32, f"ep{m}", m // 2 % 3)
+            ep = ep_pair[:, m % 2]
+            res = after("bf_last" if m == HG else f"site{m}", [P, NT], F32, f"res{m}")
+            parts = 2 if m in (0, MB - 1) else 1
+            soft = vecs[:, NS + m : NS + m + 1]
             for u in range(parts):
                 cols = slice(u * NT // parts, (u + 1) * NT // parts)
-                soft = vecs[:, 0, 4 + m : 5 + m]
-                if m in VABS:
-                    nc.vector.tensor_scalar(
-                        ep[:, 2, cols], e_ps[m][:, cols], 0.0, twice[:, m : m + 1], ALU.is_ge, ALU.mult
-                    )
-                    nc.vector.scalar_tensor_tensor(
-                        ep[:, 0, cols], e_ps[m][:, cols], soft, ep[:, 2, cols], ALU.subtract, ALU.add
-                    )
-                    nc.scalar.activation(ep[:, 1, cols], ep[:, 0, cols], ACT.Abs_reciprocal_sqrt)
-                else:
-                    nc.scalar.activation(ep[:, 0, cols], e_ps[m][:, cols], ACT.Abs)
-                    nc.scalar.activation(ep[:, 1, cols], ep[:, 0, cols], ACT.Abs_reciprocal_sqrt, bias=soft)
+                nc.scalar.activation(ep[:, 0, cols], e_ps[m][:, cols], ACT.Abs)
+                nc.scalar.activation(ep[:, 0, cols], ep[:, 0, cols], ACT.Abs_reciprocal_sqrt, bias=soft)
             for u in range(parts):
                 cols = slice(u * NT // parts, (u + 1) * NT // parts)
-                if m in GSQ:
-                    nc.gpsimd.tensor_tensor(ep[:, 2, cols], ep[:, 1, cols], ep[:, 1, cols], ALU.mult)
-                    nc.vector.tensor_tensor(ep[:, 3, cols], e_ps[m][:, cols], ep[:, 2, cols], ALU.mult)
+                if m in (7,):
+                    nc.scalar.activation(ep[:, 1, cols], ep[:, 0, cols], ACT.Square)
+                    nc.vector.tensor_tensor(res[:, cols], e_ps[m][:, cols], ep[:, 1, cols], ALU.mult)
                 else:
-                    nc.vector.tensor_tensor(ep[:, 2, cols], e_ps[m][:, cols], ep[:, 1, cols], ALU.mult)
-                    nc.vector.tensor_tensor(ep[:, 3, cols], ep[:, 2, cols], ep[:, 1, cols], ALU.mult)
-                nc.sync.dma_start(out[P * m : P * (m + 1), cols], ep[:, 3, cols])
+                    nc.vector.tensor_tensor(ep[:, 1, cols], e_ps[m][:, cols], ep[:, 0, cols], ALU.mult)
+                    nc.vector.tensor_tensor(res[:, cols], ep[:, 1, cols], ep[:, 0, cols], ALU.mult)
+                nc.sync.dma_start(out[P * m : P * (m + 1), cols], res[:, cols])

@@ -89,9 +89,9 @@ def tile_list_triage_template_scores_kernel(
             nc.sync.dma_start(tab_w[a][:], tab_words[a].rearrange("p t i -> p (t i)").bitcast(I32))
 
         def load_scales(dst, src):
-            for q in range(4):
-                rows = src[:, 4 * q : 4 * q + 4, :].rearrange("a r t -> r a t")
-                nc.sync.dma_start(dst[32 * q : 32 * q + 4].bitcast(I32), rows.bitcast(I32))
+            for r in range(4):
+                rows = src.rearrange("a (q r) t -> r q a t", r=4)[r]
+                nc.sync.dma_start(dst[r:P:32].bitcast(I32), rows.bitcast(I32))
 
         def load_w1(chunk, a):
             s0, s1 = W1_CHUNKS[chunk]
@@ -155,7 +155,10 @@ def tile_list_triage_template_scores_kernel(
                 w1_q[s] = ringed([P, KP * P], U32, f"w1_q{s}", "w1_q", 6)
                 w1_sc[s] = ringed([P, KP * P], U8, f"w1_sc{s}", "w1_sc", 6)
             for a in range(a0, a1):
-                copy(w1_bf[:, a - a0], w1_raw[s, a].rearrange("p j c -> p c j"))
+                copy(
+                    w1_bf[:, a - a0].rearrange("p (c i) j -> p c j i", i=4),
+                    w1_raw[s, a].rearrange("p j (c i) -> p c j i", i=4),
+                )
             nc.vector.quantize_mx(
                 out=w1_q[s][:, P * a0 : P * a1].bitcast(E4M3X4),
                 scales=w1_sc[s][:, P * a0 : P * a1],

from contextlib import ExitStack

import concourse.mybir as mybir
from concourse.masks import make_identity

K, H, T, S, T2, NT = 1536, 1024, 2048, 512, 1024, 512
FLOPS = 2 * (2 * K * H * S + H * T2 * NT)

F32 = mybir.dt.float32
BF16 = mybir.dt.bfloat16
I32 = mybir.dt.int32
U32 = mybir.dt.uint32
U16 = mybir.dt.uint16
U8 = mybir.dt.uint8
E4M3X4 = mybir.dt.float8_e4m3fn_x4
E2M1X4 = mybir.dt.float4_e2m1fn_x4
ACT = mybir.ActivationFunctionType
ALU = mybir.AluOpType

P = 128
KP = K // 512
RP = H // 512
NS = H // P
MB = T2 // P
JB = NT // P
W1_CHUNKS = ((0, 1), (1, 2), (2, 4), (4, 6), (6, 8))
VCAST = -1 + 1
FIRST = 1
BFB = 4
EM = 0
ET = "..atgatg"
GB = 1
HG = 3
H_OWN = {HG: "bf_last"}
H_AFTER = ("h0", "h1", "h0", "h1", "h0", "h1", "woven6", "woven7")
BF_AFTER = ("b0", "b1", "b0", "b1", "b0", "b1", "b0", "b1")


def tile_list_triage_template_scores_kernel(
    tc, tab_words, tab_scales, offs, offs2, offs3, w1, w4_words, w4_scales, site, wgs, page0, tvec, slot, out
):
    nc = tc.nc
    with ExitStack() as ctx:
        keep = ctx.enter_context(tc.tile_pool(name="keep", bufs=1))
        big = ctx.enter_context(tc.tile_pool(name="big", bufs=1))
        ring = ctx.enter_context(tc.tile_pool(name="ring", bufs=2))
        psum = ctx.enter_context(tc.psum_pool(name="psum", bufs=2))

        def kept(shape, dtype, name):
            return keep.tile(shape, dtype, name=name, align_bytes=64)

        def after(tenant, shape, dtype, name):
            return keep.tile(shape, dtype, name=name, tag=tenant, align_bytes=64)

        def big_tile(shape, dtype, name, place):
            return big.tile(shape, dtype, name=name, tag=f"place{place}", align_bytes=64)

        def ringed(shape, dtype, name, tag, bufs):
            return ring.tile(shape, dtype, name=name, tag=tag, bufs=bufs, align_bytes=64)

        def bank(tag, name):
            return psum.tile([P, 512], F32, name=name, tag=tag)[:]

        def two_banks(name):
            both = psum.tile([P, 2, 512], F32, name=name, tag="double", bufs=1)
            return both[:, 0, :], both[:, 1, :]

        list1 = keep.tile([P, S // 16], U16, name="list1")
        list2 = keep.tile([P, S // 16], U16, name="list2")
        list3 = keep.tile([P, NT // 16], U16, name="list3")
        tab_sc = kept([P, KP, T], U8, "tab_sc")
        w4_sc = kept([P, KP, H], U8, "w4_sc")
        vec_rows = after("mx0", [P, P], F32, "vec_rows")
        ident = kept([P, P], F32, "ident")
        ident_bf = kept([P, P], BF16, "ident_bf")
        wgs_sb = kept([P, S], F32, "wgs_sb")
        nc.vector.memset(tab_sc[:].rearrange("p a t -> p (a t)").bitcast(I32), 0)
        nc.vector.memset(w4_sc[:].rearrange("p a t -> p (a t)").bitcast(I32), 0)
        nc.vector.memset(vec_rows[:], 0.0)
        make_identity(nc, ident[:])
        make_identity(nc, ident_bf[:])
        warm0 = kept([P, 1], F32, "warm0")
        nc.scalar.activation(warm0[:], ident[:, 0:1], ACT.Sigmoid)

        tab_w, w1_raw, w4_w, site_sb, page = {}, {}, {}, {}, {}

        def load_tab(a):
            tab_w[a] = big_tile([P, T], I32, f"tab_w{a}", a)
            nc.sync.dma_start(tab_w[a][:], tab_words[a].rearrange("p t i -> p (t i)").bitcast(I32))

        def load_scales(dst, src):
            for r in range(4):
                rows = src.rearrange("a (q r) t -> r q a t", r=4)[r]
                nc.sync.dma_start(dst[r:P:32].bitcast(I32), rows.bitcast(I32))

        def load_w1(chunk, a):
            s0, s1 = W1_CHUNKS[chunk]
            place = a if chunk == 3 else f"{chunk}{a}"
            raw = big_tile([P, 4, P * (s1 - s0)], F32, f"w1_raw{chunk}{a}", place)
            src = w1[512 * a : 512 * (a + 1), P * s0 : P * s1]
            nc.sync.dma_start(raw[:], src.rearrange("(p j) c -> p j c", j=4))
            for s in range(s0, s1):
                w1_raw[s, a] = raw[:, :, P * (s - s0) : P * (s - s0 + 1)]

        def load_w4(b):
            w4_w[b] = kept([P, KP, 1024], U8, f"w4_w{b}")
            src = w4_words[:, :, 1024 * b : 1024 * (b + 1)].rearrange("a p c -> p a c")
            nc.sync.dma_start(w4_w[b][:].bitcast(I32), src.bitcast(I32))

        def load_site(s):
            site_sb[s] = after(f"site{s}", [P, S], F32, f"site{s}")
            nc.sync.dma_start(site_sb[s][:], site[P * s : P * (s + 1), :])

        def load_page(s):
            page[s] = kept([P, T2], F32, f"page{s}")
            nc.sync.dma_start(page[s][:], page0[P * s : P * (s + 1), :])

        nc.sync.dma_start(list1[:], offs)
        load_tab(0)
        load_scales(tab_sc, tab_scales)
        load_tab(1)
        load_scales(w4_sc, w4_scales)
        load_w4(0)
        load_tab(2)
        for a in range(KP):
            load_w1(0, a)
        load_site(0)
        nc.sync.dma_start(wgs_sb[:], wgs)
        nc.sync.dma_start(list2[:], offs2)
        load_page(0)
        load_w4(1)
        for a in range(KP):
            load_w1(1, a)
        nc.sync.dma_start(list3[:], offs3)

        v_w, v_sc = {}, {}

        def gather_table(a):
            v_w[a] = kept([P, S], U32, f"v_w{a}")
            nc.vector.tensor_copy(v_w[a][:], tab_w[a][:].bitcast(U32).indirect(list1[:]))
            v_sc[a] = kept([P, S], U8, f"v_sc{a}")
            nc.vector.tensor_copy(v_sc[a][:], tab_sc[:, a, :].indirect(list1[:]))

        w1_q, w1_sc, bf_last = {}, {}, []

        def quant_w1_part(s, a0, a1):
            copy = nc.vector.tensor_copy if s < VCAST else nc.scalar.copy
            if s < NS - 1:
                w1_bf = ringed([P, a1 - a0, P, 4], BF16, f"w1_bf{s}{a0}", f"w1_bf{a0}", BFB)[:]
            else:
                if a0 == 0:
                    bf_last.append(after("bf_last", [P, KP, P, 4], BF16, "w1_bf_last"))
                w1_bf = bf_last[0][:, a0:a1]
            if a0 == 0:
                w1_q[s] = ringed([P, KP * P], U32, f"w1_q{s}", "w1_q", 6)
                w1_sc[s] = ringed([P, KP * P], U8, f"w1_sc{s}", "w1_sc", 6)
            for a in range(a0, a1):
                copy(
                    w1_bf[:, a - a0].rearrange("p (c i) j -> p c j i", i=4),
                    w1_raw[s, a].rearrange("p j (c i) -> p c j i", i=4),
                )
            nc.vector.quantize_mx(
                out=w1_q[s][:, P * a0 : P * a1].bitcast(E4M3X4),
                scales=w1_sc[s][:, P * a0 : P * a1],
                in_=w1_bf.rearrange("p a c j -> p (a c j)"),
            )

        def quant_w1(s):
            quant_w1_part(s, 0, 2)
            quant_w1_part(s, 2, 3)

        gate, a_ps, h_sb, picked, pair = {}, {}, {}, {}, {}

        def gate_of(s):
            b, t = divmod(s, 4)
            acc = bank("g", f"b_ps{s}")
            for a in range(KP):
                nc.tensor.matmul_mx(
                    out=acc[:],
                    lhsT=w4_w[b][:, a, 256 * t : 256 * (t + 1)].bitcast(E2M1X4),
                    lhsT_scale=w4_sc[:, a, P * s : P * (s + 1)],
                    rhs=v_w[a][:].bitcast(E4M3X4),
                    rhs_scale=v_sc[a][:],
                    start=(a == 0),
                    stop=(a == KP - 1),
                )
            gate[s] = after(f"gate{s}", [P, S], F32, f"gate{s}")
            nc.scalar.activation(gate[s][:], acc[:], ACT.Sigmoid)

        def first_product(s):
            a_ps[s] = bank("a" if s % 4 < 2 else "g", f"a_ps{s}")
            for a in range(KP):
                nc.tensor.matmul_mx(
                    out=a_ps[s][:],
                    lhsT=w1_q[s][:, P * a : P * (a + 1)].bitcast(E4M3X4),
                    lhsT_scale=w1_sc[s][:, P * a : P * (a + 1)],
                    rhs=v_w[a][:].bitcast(E4M3X4),
                    rhs_scale=v_sc[a][:],
                    start=(a == 0),
                    stop=(a == KP - 1),
                )

        def gate_site(s):
            nc.vector.tensor_tensor(site_sb[s][:], site_sb[s][:], gate[s][:], ALU.mult)

        def make_h(s):
            h_sb[s] = after(H_OWN[s], [P, S], F32, f"h{s}")[:] if s in H_OWN else site_sb[s][:]
            nc.vector.tensor_tensor(h_sb[s], a_ps[s][:], site_sb[s][:], ALU.add)

        def scatter(s):
            nc.vector.tensor_tensor(page[s][:].indirect(list2[:]), h_sb[s], wgs_sb[:], ALU.mult)

        def pick(s):
            picked[s] = after(f"gate{s}", [P, NT], F32, f"picked{s}")[:]
            nc.vector.tensor_copy(picked[s], page[s][:].indirect(list3[:]))

        for a in range(KP):
            gather_table(a)
            if a == 0:
                quant_w1(0)
        gate_of(0)
        first_product(0)
        gate_site(0)
        make_h(0)

        load_site(1)
        for a in range(KP):
            load_w1(2, a)
        load_page(1)
        load_site(2)
        for a in range(KP):
            load_w1(3, a)
        load_page(2)
        for a in range(KP):
            load_w1(4, a)
        load_site(3)
        nc.sync.dma_start(vec_rows[0:NS, :], tvec.rearrange("(s p) -> s p", p=P))
        nc.sync.dma_start(vec_rows[NS : NS + MB, :], slot.rearrange("(s p) -> s p", p=P))
        load_page(3)
        load_site(4)
        load_page(4)
        load_site(5)
        load_page(5)
        load_site(6)
        load_page(6)
        load_site(7)
        load_page(7)

        vecs = {}


        page_T = {(b, h): kept([P, 4, 2, P, 2], BF16, f"page_T{b}{h}") for b in range(RP) for h in range(2)}
        x_T = {b: kept([P, JB, 2, P], F32, f"x_T{b}") for b in range(RP)}
        x_bf, pg_bf = {}, {}
        x_q = {1: kept([P, NT], U32, "x_q1")[:]}
        x_sc = [kept([P, NT], U8, f"x_sc{b}") for b in range(RP)]
        pg_q = {(1, c): kept([P, 2 * P], U32, f"pg_q1{c}")[:] for c in range(MB // 2)}
        pg_sc = {(b, c): kept([P, 2 * P], U8, f"pg_sc{b}{c}") for b in range(RP) for c in range(MB // 2)}

        def turn_page(s, h, turned):
            b, t = divmod(s, 4)
            for i in range(4):
                m0 = P * (4 * h + i)
                nc.tensor.transpose(turned[:, P * i : P * (i + 1)], page[s][:, m0 : m0 + P], ident[:])
            copy = nc.vector.tensor_copy if s == NS else nc.scalar.copy
            copy(
                page_T[b, h][:, :, :, 32 * t : 32 * (t + 1), :],
                turned[:].rearrange("p (i q u e) -> p i u q e", i=4, u=2, e=2),
            )

        def turn_x(s, between):
            b, t = divmod(s, 4)
            mag = after("mx0", [P, NT], F32, f"mag{s}")
            nc.scalar.activation(mag[:], picked[s], ACT.Abs)
            places = ("xf0", "codes0") if s == NS - 2 else (f"xf{s % 2}",)
            width = NT // len(places)
            x_flat = [after(place, [P, width], BF16, f"x_flat{s}{place}") for place in places]
            for c, part in enumerate(x_flat):
                nc.scalar.activation(part[:], mag[:, width * c : width * (c + 1)], ACT.Copy, scale=vecs[:, s : s + 1])
            between()
            turned = two_banks(f"x_ps{s}")[0] if s < NS - 1 else bank("a", f"x_ps{s}")
            for i in range(JB):
                nc.tensor.transpose(
                    turned[:].bitcast(BF16)[:, P * i : P * (i + 1)], x_flat[P * i // width][:, P * i % width : P * i % width + P], ident_bf[:]
                )
            nc.scalar.copy(
                x_T[b][:, :, :, 32 * t : 32 * (t + 1)],
                turned[:, 0 : JB * P // 2].rearrange("p (i q u) -> p i u q", i=JB, u=2),
            )

        def turn_back(words, tag, name, copy, place):
            back = bank(tag, f"{name}_ps")
            for i in range(2):
                for u in range(2):
                    o = P * (2 * i + u)
                    nc.tensor.transpose(back[:, o : o + P], words[:, i, u, :], ident[:])
            woven = after(place, [P, 2 * P * 4], BF16, f"{name}_bf")
            copy(
                woven[:].bitcast(F32).rearrange("p (i m u) -> p i m u", i=2, u=2),
                back[:].rearrange("p (i u m) -> p i m u", i=2, u=2),
            )
            return woven

        def quantise(woven, codes, scales):
            nc.vector.quantize_mx(out=codes.bitcast(E4M3X4), scales=scales, in_=woven[:])

        def quant_x(b, c, tag, copy):
            x_bf[b, c] = turn_back(x_T[b][:, 2 * c : 2 * c + 2], tag, f"x{b}{c}", copy, f"wx{c}")
            if b == 1:
                quantise_x(b, c)

        def quantise_x(b, c):
            cols = slice(2 * P * c, 2 * P * (c + 1))
            quantise(x_bf[b, c], x_q[b][:, cols], x_sc[b][:, cols])

        def quant_page(b, c, tag, copy):
            h, i = divmod(c, 2)
            words = page_T[b, h][:].rearrange("p i u q e -> p (i u q e)").bitcast(F32)
            words = words.rearrange("p (i u q) -> p i u q", i=4, u=2)[:, 2 * i : 2 * i + 2]
            pg_bf[b, c] = turn_back(words, tag, f"pg{b}{c}", copy, f"wp{c}")
            if b == 1:
                quantise(pg_bf[b, c], pg_q[b, c], pg_sc[b, c][:])

        e_ps = {}

        def score_pass(m, b, cols, start, stop):
            c, i = divmod(m, 2)
            nc.tensor.matmul_mx(
                out=e_ps[m][:, cols],
                lhsT=pg_q[b, c][:, P * i : P * (i + 1)].bitcast(E4M3X4),
                lhsT_scale=pg_sc[b, c][:, P * i : P * (i + 1)],
                rhs=x_q[b][:, cols].bitcast(E4M3X4),
                rhs_scale=x_sc[b][:, cols],
                start=start,
                stop=stop,
            )

        for s in range(1, NS):
            gate_of(s)
        for s in range(1, NS):
            quant_w1(s)
        warm = kept([P, 1], F32, "warm")
        nc.scalar.activation(warm[:], gate[NS - 1][:, 0:1], ACT.Abs_reciprocal_sqrt)
        for s in range(1, NS):
            first_product(s)
            gate_site(s)
            make_h(s)
            scatter(s - 1)
            pick(s - 1)
        scatter(NS - 1)
        vecs = after(f"site{HG}", [P, NS + MB], F32, "vecs")
        for c0, c1 in ((0, NS), (NS, NS + MB)):
            vec_T = bank("t", f"vec_T{c0}")
            nc.tensor.transpose(vec_T[:, 0:P], vec_rows[:], ident[:])
            nc.scalar.copy(vecs[:, c0:c1], vec_T[:, c0:c1])
        for s in range(NS - 1):
            if s == 4:
                for c in range(MB // 2):
                    quant_page(0, c, "a", nc.scalar.copy)
                for c in range(2):
                    quant_x(0, c, "a", nc.scalar.copy)
            banks = (bank("t", f"page_ps{s}0"), bank("t", f"page_ps{s}1"))
            turn_page(s, 0, banks[0])
            turn_x(s, lambda: turn_page(s, 1, banks[1]))

        last = NS - 1
        half = NT // 2
        picked_last = after("xf0", [P, NT], F32, "picked_last")
        mag_last = after("mx0", [P, NT], F32, "mag_last")
        x_last = after("xf1", [P, NT], BF16, "x_last")
        banks = two_banks("last_ps")
        for c in range(2):
            cols = slice(half * c, half * (c + 1))
            offsets = list3[:, half // 16 * c : half // 16 * (c + 1)]
            nc.vector.tensor_copy(picked_last[:, cols], page[last][:].indirect(offsets))
            nc.scalar.activation(mag_last[:, cols], picked_last[:, cols], ACT.Abs)
        for c in range(2):
            cols = slice(half * c, half * (c + 1))
            nc.vector.tensor_scalar(x_last[:, cols], mag_last[:, cols], vecs[:, last : last + 1], None, ALU.mult)
            turned = bank("a", f"x_last_ps{c}")
            for i in range(2):
                j0 = half * c + P * i
                nc.tensor.transpose(turned.bitcast(BF16)[:, P * i : P * (i + 1)], x_last[:, j0 : j0 + P], ident_bf[:])
            nc.vector.tensor_copy(
                x_T[1][:, 2 * c : 2 * c + 2, :, 96:128],
                turned[:, 0:P].rearrange("p (i q u) -> p i u q", i=2, u=2),
            )
        turn_page(last, 0, banks[0])
        turn_page(last, 1, banks[1])
        codes0 = after("codes0", [P, NT + T2], U32, "codes0")
        x_q[0] = codes0[:, 0:NT]
        for c in range(MB // 2):
            pg_q[0, c] = codes0[:, NT + 2 * P * c : NT + 2 * P * (c + 1)]
        for c in range(2):
            quantise_x(0, c)
        for c in range(MB // 2):
            quantise(pg_bf[0, c], pg_q[0, c], pg_sc[0, c][:])
        quant_x(1, 0, "g", nc.vector.tensor_copy)
        quant_page(1, 0, "t", nc.scalar.copy)
        quant_x(1, 1, "g", nc.scalar.copy)
        quant_page(1, 1, "t", nc.vector.tensor_copy)
        quant_page(1, 2, "a", nc.scalar.copy)
        quant_page(1, 3, "a", nc.scalar.copy)
        for m in range(MB):
            if m == EM:
                e_ps[m], e_ps[m + 1] = two_banks("e_pair")
            elif m != EM + 1:
                e_ps[m] = bank(ET[m], f"e_ps{m}")
            groups = 2 if m == 0 else 1
            for u in range(groups):
                cols = slice(u * NT // groups, (u + 1) * NT // groups)
                score_pass(m, FIRST, cols, True, False)
                score_pass(m, 1 - FIRST, cols, False, True)
            if m % 2 == 0:
                ep_pair = big_tile([P, 2, 2, NT], F32, f"ep{m}", m // 2 % 3)
            ep = ep_pair[:, m % 2]
            res = after("bf_last" if m == HG else f"site{m}", [P, NT], F32, f"res{m}")
            parts = 2 if m in (0, MB - 1) else 1
            soft = vecs[:, NS + m : NS + m + 1]
            for u in range(parts):
                cols = slice(u * NT // parts, (u + 1) * NT // parts)
                nc.scalar.activation(ep[:, 0, cols], e_ps[m][:, cols], ACT.Abs)
                nc.scalar.activation(ep[:, 0, cols], ep[:, 0, cols], ACT.Abs_reciprocal_sqrt, bias=soft)
            for u in range(parts):
                cols = slice(u * NT // parts, (u + 1) * NT // parts)
                if m in (7,):
                    nc.scalar.activation(ep[:, 1, cols], ep[:, 0, cols], ACT.Square)
                    nc.vector.tensor_tensor(res[:, cols], e_ps[m][:, cols], ep[:, 1, cols], ALU.mult)
                else:
                    nc.vector.tensor_tensor(ep[:, 1, cols], e_ps[m][:, cols], ep[:, 0, cols], ALU.mult)
                    nc.vector.tensor_tensor(res[:, cols], ep[:, 1, cols], ep[:, 0, cols], ALU.mult)
                nc.sync.dma_start(out[P * m : P * (m + 1), cols], res[:, cols])
